import numpy as np, ml_dtypes
CORES = [66,74,82,90,194,202,210,218]
N = 8
BF = ml_dtypes.bfloat16
def gentries(a):
    return np.ascontiguousarray(a.reshape(8, 16, -1).transpose(0, 2, 1)).reshape(8, -1)
def gtable(e):
    e = np.asarray(e); return np.ascontiguousarray(e.reshape(8, -1, 16).transpose(0, 2, 1)).reshape(128, -1).astype(np.int32)
W0, B, LN, RO, SP, CAP = 2048, 128, 1536, 2, 4, 384
W = W0 + RO * B
def parts(rng):
    scale = np.array([0.5, 1, 1.5, 2, 3, 4, 6, 8])[np.argsort(rng.random((N, 8)), axis=1)][:, :, None, None]; dens = 0.1 + 0.6 * rng.random((N, 8, 1, W0))
    cnt = np.where(rng.random((N, 8, 16, W0)) < dens, np.minimum(15, 1 + (scale * rng.standard_exponential((N, 8, 16, W0))).astype(np.int64)), 0)
    hot = rng.integers(0, W0, (N, 8, 64))
    def some(n, share):
        return np.where(rng.random((N, 8, n)) < share, np.take_along_axis(hot, rng.integers(0, 64, (N, 8, n)), 2), rng.integers(0, W0, (N, 8, n)))
    ptr = some(16 * W0, 0.4).reshape(N, 8, 16, W0); suf = (np.arange(W0) * rng.random((N, 8, W0))).astype(np.int64)
    return cnt, ptr, suf, rng.integers(0, W0, (N, 8, W0)), some(LN, 0.3), rng.integers(0, 256, (N, 8, RO * SP, LN))
def levels(rng, cnt, suf, v, g):
    x = np.arange(W0); b = np.where(x <= 16, 3, np.where(x <= 32, 2, np.where(x <= 48, 1, 0)))
    cnt[:, g] = np.where((np.arange(16) >> 2)[:, None] == b, rng.integers(1, 16, (N, 16, W0)), 0)
    suf[:, g] = rng.integers(1, 17, (N, W0)) + 16 * np.maximum(2 - b, 0)
    v[:, g, :SP - 1, :B] = rng.integers(240, 256, (N, SP - 1, B)); v[:, g, SP - 1, :B] = rng.integers(0, 128, (N, B))
def clones(rng, cnt, ptr, suf, lnk, cx, v, g):
    o = 1 + np.argsort(rng.random((N, W0 - 1)), axis=1); x = o[:, :B]; b = o[:, B:2 * B]; u = o[:, 2 * B:3 * B]
    qi = np.arange(N)[:, None]; z = rng.integers(1, 16, (N, B)); ct = cnt[:, g]; pt = ptr[:, g]
    for y in (x, u):
        ct[qi, :, y] = 0; ct[qi, 0, y] = 1; pt[qi, 0, y] = y
    ct[qi, :, b] = 0; ct[qi, z, b] = 1; pt[qi, z, b] = u
    suf[qi, g, x] = b; suf[qi, g, u] = x; lnk[qi, g, u] = np.maximum(lnk[qi, g, u], 1); cx[:, g, :B] = x
    v[:, g, :, :B] = rng.integers(0, 64, (N, RO * SP, B))
    for s in (SP - 2, 2 * SP - 2): v[:, g, s, :B] = rng.integers(128, 256, (N, B))
    if (RO - 2) * SP > 2:
        v[:, g, RO * SP - 2, :B] = rng.integers(64, 128, (N, B)); v[:, g, RO * SP - 1, :B] = rng.integers(128, 256, (N, B))
def kept(rng, cnt, ptr, suf, cx, v, g):
    o = 1 + np.argsort(rng.random((N, W0 - 1)), axis=1)[:, :(SP + 1) * B]; h = o[:, :SP * B]; b = o[:, SP * B:]
    qi = np.arange(N)[:, None]; z = rng.integers(1, 16, (N, B)); ct = cnt[:, g]; pt = ptr[:, g]
    ct[qi, :, h] = 0; ct[qi, 0, h] = 1; pt[qi, 0, h] = h; suf[qi, g, h] = o[:, B:]
    ct[qi, :, b] = 0; ct[qi, z, b] = 1; cx[:, g] = o[:, np.arange(LN) % B]
    v[:, g, :SP] = rng.integers(0, 128, (N, SP, LN)); v[1::2, g, SP - 1, :B] = rng.integers(128, 256, (N // 2, B))
    v[:, g, 2 * SP - 1, :B] = rng.integers(0, 128, (N, B))
def filled(rng, cnt, ptr, suf, lnk, cx, v, g):
    o = 1 + np.argsort(rng.random((N, W0 - 1)), axis=1)[:, :(2 * SP + 1) * B]; x = o[:, :B]; y = o[:, B:]; b1 = o[:, SP * B:(SP + 1) * B]; b2 = o[:, 2 * SP * B:]
    qi = np.arange(N)[:, None]; ct = cnt[:, g]; pt = ptr[:, g]
    ct[qi, :, o] = 0; ct[qi, 0, o] = 1; pt[qi, 0, o] = o
    for b, lo in ((b1, 1), (b2, 8)):
        ct[qi, 0, b] = 0; ct[qi, rng.integers(lo, lo + 7, (N, B)), b] = 1
    suf[qi, g, x] = np.roll(x, -1, axis=1); suf[qi, g, y[:, :-B]] = y[:, B:]; lnk[qi, g, x] = np.roll(y[:, :B], -1, axis=0)
    cx[:, g] = x[:, np.arange(LN) % B]
    v[:, g, :2 * SP] = rng.integers(0, 128, (N, 2 * SP, LN)); v[:, g, SP - 1, :B] = rng.integers(128, 256, (N, B))
    q4 = np.arange(N) % 4; v[:, g, 2 * SP - 1, :B // 2] += 128 * ((q4 == 1) | (q4 == 2))[:, None]
    if RO > 2: v[:, g, 3 * SP - 1, :B // 2] = rng.integers(0, 128, (N, B // 2))
def pack(cnt, ptr, suf, lnk, cx, v):
    return {"tab": np.ascontiguousarray((16 * ptr + cnt).reshape(N, 128, W0)).astype(np.int32), "suf": suf.astype(np.int32), "lnk": lnk.astype(np.int32),
            "cx": np.stack([gtable(a) for a in cx]), "vv": v.reshape(N, 8, RO * SP * LN).astype(np.float32).astype(BF)}
def setup_inputs(rng):
    return pack(*parts(rng))
def setup_inputs_room(rng):
    cnt, ptr, suf, lnk, cx, v = parts(rng)
    cnt = np.where(np.arange(16)[:, None] == rng.integers(0, 16, (N, 8, 1, W0)), np.maximum(cnt, 1), cnt); ptr = np.maximum(ptr, 1); cx = np.maximum(cx, 1)
    v[:, :, :SP - 1] = rng.integers(0, 128, (N, 8, SP - 1, LN)); opts = (0, 1, CAP - 1, CAP, CAP + 1, LN)
    for q in range(N):
        o = rng.permutation(6)
        for g in range(6):
            m = opts[g] if q == 0 else opts[5 - g] if q == 1 else opts[int(o[g])]
            v[q, g, SP - 1] = np.where(rng.permutation(LN) < m, rng.integers(240, 256, LN), rng.integers(0, 128, LN))
    for g in (6, 7):
        levels(rng, cnt, suf, v, g)
        for q in range(N): cx[q, g, :B] = 64 + rng.permutation(W0 - 64)[:B]
    return pack(cnt, ptr, suf, lnk, cx, v)
def setup_inputs_ties(rng):
    cnt, ptr, suf, lnk, cx, v = parts(rng)
    rows = np.array([4, 1, 2, 8, 1, 0, 16, 4, 8, 8, 16]); vals = np.array([3, 1, 1, 1, 15, 0, 15, 1, 3, 7, 3]); k = rng.integers(0, 11, (N, 8, W0))
    order = np.argsort(rng.random((N, 8, W0, 16)), axis=-1)
    cnt = np.where(order < rows[k][..., None], vals[k][..., None], 0).transpose(0, 1, 3, 2)
    v = np.where(rng.random(v.shape) < 0.6, 16 * rng.integers(0, 17, v.shape), 15 * rng.integers(0, 18, v.shape)) + np.where(rng.random(v.shape) < 0.6, 0, rng.integers(-1, 2, v.shape))
    return pack(cnt, ptr, suf, lnk, cx, np.minimum(np.maximum(v, 0), 255))
def setup_inputs_alike(rng):
    cnt, ptr, suf, lnk, cx, v = parts(rng); few = rng.integers(1, W0, (N, 8, 6))
    def some(n, m):
        return np.take_along_axis(few, rng.integers(0, m, (N, 8, n)), 2)
    ptr = some(16 * W0, 6).reshape(N, 8, 16, W0); suf = np.where(rng.random((N, 8, W0)) < 0.5, some(W0, 6), suf); lnk = np.where(rng.random((N, 8, W0)) < 0.5, some(W0, 6), lnk); cx = some(LN, 4)
    levels(rng, cnt, suf, v, 3); cx[:, 3, :B] = rng.choice(np.array([70, W0 - 1]), (N, B))
    cx[:, 5] = cx[:, 5, :1]; v[:, 5] = v[:, 5, :, :1]
    filled(rng, cnt, ptr, suf, lnk, cx, v, 2); kept(rng, cnt, ptr, suf, cx, v, 6); clones(rng, cnt, ptr, suf, lnk, cx, v, 7)
    return pack(cnt, ptr, suf, lnk, cx, v)
def setup_inputs_ends(rng):
    cnt, ptr, suf, lnk, cx, v = parts(rng); e = np.array([0, 1, W0 - 1])
    ptr = np.where(rng.random(ptr.shape) < 0.3, rng.choice(e, ptr.shape), ptr); lnk = np.where(rng.random(lnk.shape) < 0.5, rng.choice(e, lnk.shape), lnk); cx = np.where(rng.random(cx.shape) < 0.5, rng.choice(e, cx.shape), cx)
    suf[:, 1::2] = np.where(rng.random((N, 4, W0)) < 0.3, np.arange(W0), rng.integers(0, W0, (N, 4, W0))); suf[:, 2] = 0; suf[:, 4] = 0; suf[:, 5] = 0
    cnt[:, 4, :, 0] = 0; cnt[:, 5, :, 0] = 15; cnt[:, 6] = 15 * (cnt[:, 6] > 0); cnt[:, 7, :, W0 - 1] = 0; cnt[:, 0, :, W0 - 1] = 15
    v = np.where(rng.random(v.shape) < 0.7, rng.choice(np.array([0, 1, 127, 128, 239, 240, 254, 255]), v.shape), v)
    return pack(cnt, ptr, suf, lnk, cx, v)
def setup_inputs_spread(rng):
    def low(*shape):
        return np.minimum((W0 * rng.random(shape) ** rng.integers(1, 5, shape[:2] + (1,) * (len(shape) - 2))).astype(np.int64), W0 - 1)
    cnt = np.where(rng.random((N, 8, 16, W0)) < rng.random((N, 8, 1, W0)) ** 2, np.minimum(np.exp2(4 * rng.random((N, 8, 16, W0)) * rng.random((N, 8, 1, W0)) ** 0.5).astype(np.int64), 15), 0)
    v = np.minimum((256 * rng.random((N, 8, RO * SP, LN)) ** 3).astype(np.int64), 255)
    return pack(cnt, low(N, 8, 16, W0), low(N, 8, W0), W0 - 1 - low(N, 8, W0), low(N, 8, LN), np.where(rng.random(v.shape) < 0.5, v, 255 - v))
def check_inputs(d):
    bad = []
    for k, hi in (("tab", 16 * W0 - 1), ("suf", W0 - 1), ("lnk", W0 - 1), ("cx", W0 - 1)):
        if np.min(d[k]) < 0 or np.max(d[k]) > hi: bad.append("range of " + k)
    v = np.asarray(d["vv"]).astype(np.float32)
    if not np.all((v >= 0) & (v <= 255) & (v == np.floor(v))): bad.append("range of vv")
    return bad
def reference(tab, suf, lnk, cx, vv):
    k = tab.astype(np.int32).reshape(N, 8, 16, W0)
    C = np.zeros((N, 8, 16, W), np.int32); S = np.zeros((N, 8, 16, W), np.int32); C[..., :W0] = k & 15; S[..., :W0] = k >> 4
    F = np.zeros((N, 8, W), np.int32); L = np.zeros((N, 8, W), np.int32); F[..., :W0] = suf; L[..., :W0] = lnk
    v = vv.astype(np.float32).astype(np.int32).reshape(N, 8, RO, SP, 1, LN)
    c = np.stack([gentries(a) for a in cx]).astype(np.int32); e = np.zeros((N, 8, 16, LN), np.int32); f = np.full((N, 8, LN), -1, np.int32)
    qi = np.arange(N)[:, None, None]; gi = np.arange(8)[None, :, None]
    for t in range(RO):
        for s in range(SP):
            cc = np.take_along_axis(C, c[:, :, None, :], 3)
            n = cc * (1 - e); P = np.add.accumulate(n, axis=2, dtype=np.int32); E = np.add.reduce((n > 0).astype(np.int32), axis=2)
            z = np.add.reduce((256 * P <= v[:, :, t, s] * (P[:, :, 15] + E)[:, :, None, :]).astype(np.int32), axis=2)
            z = np.where(c == 0, np.minimum(z, 15), z); esc = z == 16
            d, fb = c, f
            f = np.where(esc, np.where(fb < 0, d, fb), -1)
            e = np.where(esc[:, :, None, :], np.maximum(e, (cc > 0).astype(np.int32)), 0)
            c = np.where(esc, F[qi, gi, d], S[qi, gi, np.minimum(z, 15), d])
        for q in range(N):
            for g in range(8):
                j = np.nonzero(~esc[q, g, :B] & (fb[q, g, :B] >= 0))[0]
                a = j[np.unique(fb[q, g, j], return_index=True)[1]]
                w = W0 + B * t + a; to = c[q, g, a]
                cw = (C[q, g][:, to] + 1) >> 1; sw = S[q, g][:, to]
                C[q, g][:, w] = cw; S[q, g][:, w] = sw; F[q, g, w] = to; L[q, g, w] = L[q, g, to]
                C[q, g, z[q, g, a], fb[q, g, a]] = 1; S[q, g, z[q, g, a], fb[q, g, a]] = w
                b = j[np.unique(d[q, g, j], return_index=True)[1]]
                C[q, g, z[q, g, b], d[q, g, b]] = np.minimum(15, C[q, g, z[q, g, b], d[q, g, b]] + 1)
        slot = esc & (np.add.accumulate(esc.astype(np.int32), axis=2) <= CAP)
        c2 = np.array(c); e2 = np.array(e); f2 = np.array(f)
        for r in range(N):
            q = (r - 1) % N
            for g in range(8):
                a = np.nonzero(slot[q, g])[0]; b = np.nonzero(slot[r, g])[0]; m = min(len(a), len(b)); a = a[:m]; b = b[:m]
                c2[r, g, b] = L[q, g, c[q, g, a]]; e2[r, g][:, b] = e[q, g][:, a]; f2[r, g, b] = -1
        c, e, f = c2, e2, f2
    return {"yn": C.reshape(N, 128, W).astype(np.float32).astype(BF), "yc": np.stack([gtable(a) for a in c]).astype(np.float32)}

@@ -1,0 +1,613 @@
+from concourse.mybir import AluOpType, ActivationFunctionType
+
+OP = AluOpType
+AF = ActivationFunctionType
+RO, SP = 2, 4
+NW = 2560
+H = 768
+F32, B16, I32, F16, U16 = "float32", "bfloat16", "int32", "float16", "uint16"
+SCRATCH = {}
+WHERE = {}
+
+
+def sb(dtype, **kw):
+    for name, n in kw.items():
+        SCRATCH[name] = ("sbuf", [128, n], dtype)
+
+
+def pool(buf, dtype, **kw):
+    o = 0
+    for name, n in kw.items():
+        WHERE[name] = (buf, o, n)
+        o += -(-n // 16) * 16
+    SCRATCH[buf] = ("sbuf", [128, o], dtype)
+
+
+sb(I32, tabI=2048, CI=2048, CPI=544, CPL=544)
+sb(F32, YB=2048, ST=NW, DT=NW, Y0=H, Y1=H, LBB=H, SW=1920)
+sb(B16, W1=2048, WT=NW, AUX=NW, VV=12288, w0=H, w1=H, n0=H, n1=H, x0=H, x1=H, k0=H, k1=H, MM=1920, YN=2304, BIT=10240, LBA=H,
+   VW=1920, A2=1536, SND0=792, SND1=792, RCV0=792, RCV1=792, LW=1920, SELK=1024, NSELK=1024, EQF=1024, EQD=1024, ABD=1024,
+   COMB=1440, ZB=1536)
+sb(F16, X0=H, X1=H, COMBX=144)
+sb(U16, CL=960)
+pool("zi", I32, CXI=96, CIT=96, i_rm=16, i_pc=16, i_g8=8, i_bm=128, i_dp=128, i_wr=128, i_k=128, i_u=128)
+pool("zf", F32, RM=16, PC=1, G8=8, SH32=128, JI=96, JL=96, J2=96, J3=96, JD=24, JD2=24, DUM0=16, DUM1=16, CLF=96, YC=96, HT=40,
+     DL=40, hd=40, d1=40, FS=40, KT=16, KT2=16, KK=16, CAND=16, CS=104, Z96=96, CNT=96, OKT=96, TT=96, TT2=96, POSF=96, PRE=24,
+     LNF=24, T1=24, RX1=24, RX2=24, AO=8, AO2=8, BO=8, BO2=8, HF=8, xs=128, kk=128, K8=8, NK8=8, COLS=64, ZF=512, d0c=1)
+pool("zb", B16, BM=128, IDN=128, NI=128, LT=128, LTB=128, TRI=128, R15=128, ESC=128, CANDM=128, BID=128, N01=128, NI2K=128,
+     U1=128, U2=128, LTu=128, ONES=128, OB=240, SWb=384, E16=96, HB=544, LB=544, XF=256, XC=128, AR=256, OH=128, OA=128, nOA=128,
+     OA2=128, OBm=128, OBm2=128, tg=128, s1=128, s2=128, s3=128, ug=128, FLs=128, fd=128, xt=128)
+pool("zh", F16, SH16=128, WR=128, tS=128, qS=128, Sc=128)
+pool("zu", U16, POS=96, LNE=24, TO=24, FK=16, OFF=8, OFD=8)
+for nm, nc in (("PA", 1536), ("PB", 1536), ("LAp", 512), ("LBp", 512)):
+    SCRATCH[nm] = ("psum", [128, nc], F32)
+
+SEMAPHORES = ["v", "s", "t", "q", "arr0", "arr1", "snt0", "snt1"] + ["d%d" % i for i in range(60)]
+CA, CE, CF, CID, CSA, CSB, CLK, C0, C7, C8 = range(10)
+
+
+def rank_program(g, core, T, topo):
+    rank = T.rank_of(core)
+    if rank is None:
+        return
+    Q = {"v": g.vector, "s": g.scalar, "t": g.tensor, "q": g, "y": g.sync}
+    cnt = {"v": 0, "s": 0, "t": 0, "q": 0}
+    know = {q: {} for q in Q}
+    res, acc, used, nd = {}, {}, {}, [0]
+
+    def do_waits(q, R, W):
+        deps = []
+        for k in R:
+            if k[0] != "#":
+                deps += res.get(k, ([], []))[0]
+        for k in W:
+            if k[0] != "#":
+                ws, rs = res.get(k, ([], []))
+                deps += ws + [e for e in rs if e[0] != q]
+        for k in list(R) + list(W):
+            if k[0] == "#":
+                deps += [e for e in acc.get(k, []) if e[0] != q]
+        best = {}
+        for e in deps:
+            if know[q].get(e[1], 0) < e[2] and (e[1] not in best or best[e[1]][2] < e[2]):
+                best[e[1]] = e
+        for e in [e for e in best.values() if not any(o is not e and o[3].get(e[1], 0) >= e[2] for o in best.values())]:
+            Q[q].wait_ge(T.sem[e[1]], e[2])
+            k = know[q]
+            k[e[1]] = max(k.get(e[1], 0), e[2])
+            for s, v in e[3].items():
+                k[s] = max(k.get(s, 0), v)
+
+    def record(ent, R, W):
+        for k in W:
+            if k[0] != "#":
+                res[k] = ([ent], [])
+        for k in R:
+            if k[0] != "#" and k not in W:
+                ws, rs = res.get(k, ([], []))
+                res[k] = (ws, [e for e in rs if e[0] != ent[0]] + [ent])
+        for k in list(R) + list(W):
+            if k[0] == "#":
+                acc[k] = [ent]
+
+    def op(q, R, W, *fns):
+        do_waits(q, R, W)
+        for fn in fns:
+            fn(Q[q]).then_inc(T.sem[q], 1)
+            cnt[q] += 1
+        clock = dict(know[q])
+        clock[q] = cnt[q]
+        record((q, q, cnt[q], clock), R, W)
+
+    def dma(q, R, W, *pairs):
+        do_waits(q, R, W)
+        name = "d%d" % nd[0]
+        nd[0] += 1
+        for o, i in pairs:
+            Q[q].dma_start(o, i).then_inc(T.sem[name], 16)
+        used[name] = 16 * len(pairs)
+        record((name, name, 16 * len(pairs), dict(know[q])), R, W)
+
+    def z(name, a=0, b=None, st=1):
+        buf, o, n = WHERE[name]
+        return T[buf][:, o + a:o + (n if b is None else b):st]
+
+    def ts(out, a, s1, o1, s2=None, o2=None):
+        if o2 is None:
+            return lambda e: e.tensor_scalar(out, a, s1, None, o1)
+        return lambda e: e.tensor_scalar(out, a, s1, s2, o1, o2)
+
+    def tt(out, a, b, o):
+        return lambda e: e.tensor_tensor(out, a, b, o)
+
+    def cp(out, a):
+        return lambda e: e.tensor_copy(out, a)
+
+    def ms(out, c):
+        return lambda e: e.memset(out, c)
+
+    def ac(out, a, f, **kw):
+        return lambda e: e.activation(out, a, f, **kw)
+
+    def mm(out, l, r, st, sp):
+        return lambda e: e.matmul(out, l, r, st, sp)
+
+    def V(R, W, *f):
+        op("v", R, W, *f)
+
+    def S(R, W, *f):
+        op("s", R, W, *f)
+
+    def PE(R, W, *f):
+        op("t", R, W, *f)
+
+    def tz(out, a, s1, o1, *more):
+        V([a], [out], ts(z(out), z(a), s1, o1, *more))
+
+    def t2(out, a, b, o):
+        V([a, b], [out], tt(z(out), z(a), z(b), o))
+
+    PX, LP = [T.PA, T.PB], [T.LAp, T.LBp]
+    PK0, PK2, LK = ["#A0", "#B0"], ["#A2", "#B2"], ["#LA", "#LB"]
+    w, n, x, cond, X, Y = ([T["%s%d" % (a, p)] for p in (0, 1)] for a in ("w", "n", "x", "k", "X", "Y"))
+    AUXK = ["AUX"] + ["ar%d" % i for i in range(10)]
+
+    def comb(v, i):
+        return T.COMB[:, v * 144 + 15 - i:v * 144 + 143 - i]
+
+    def combx(i):
+        return T.COMBX[:, 15 - i:143 - i]
+
+    def RMc(r):
+        return z("RM", r, r + 1)
+
+    dma("y", [], ["cpi"], (T.CPI[:, 256:384], T.suf[:, :]), (T.CPI[:, 0:128], T.tab[0:128:16, :]), (T.CPI[:, 128:256], T.lnk[:, :]))
+    for k in range(4):
+        dma("s" if k % 2 == 0 else "y", [], ["tab%d" % k], (T.tabI[:, 512 * k:512 * k + 512], T.tab[:, 512 * k:512 * k + 512]))
+    dma("y", [], ["CXI"], (z("CXI"), T.cx[:, :]))
+    dma("y", [], ["vv0"], *[(T.VV[i:128:16, 0:1536], T.vv[:, 0:1536]) for i in range(16)])
+
+    def iota(tile, key, pattern, base, cm, **kw):
+        op("q", [], [key], lambda e: e.iota(tile, pattern, base, cm, **kw))
+    fl = {"allow_small_or_imprecise_dtypes": True}
+    iota(z("i_rm"), "i_rm", [[-1, 16]], 0, 1)
+    iota(z("i_g8"), "i_g8", [[-16, 8]], 0, 1)
+    iota(z("i_bm"), "i_bm", [[-16, 8], [0, 16]], 0, 1)
+    iota(z("i_dp"), "i_dp", [[1, 128]], 0, -1)
+    iota(T.CPI[:, 384:512], "cpj", [[1, 128]], 0, 128)
+    iota(T.CPI[:, 512:544], "cpk", [[1, 32]], 0, 32)
+    iota(z("i_pc"), "i_pc", [[0, 16]], 0, 1)
+    iota(z("JI"), "JI", [[16, 96]], 0, 0, **fl)
+    iota(z("i_wr"), "i_wr", [[1, 128]], 0, 0)
+    for i in range(10):
+        iota(T.BIT[:, 1024 * i:1024 * i + 1024], "bit%d" % i, [[0, 1024 >> (i + 1)], [1, 2], [0, 1 << i]], 0, 0, **fl)
+
+    SR, BA = OP.logical_shift_right, OP.bitwise_and
+    V([], ["AUX"], ms(T.AUX[:, :], 0.0))
+    V([], ["COMB"], ms(T.COMB[:, :], 0.0))
+    V([], ["COMBX"], ms(T.COMBX[:, :], 0.0))
+    tz("i_rm", "i_rm", 15, BA)
+    tz("i_g8", "i_g8", 4, OP.arith_shift_right)
+    tz("i_bm", "i_bm", 4, OP.arith_shift_right)
+    tz("RM", "i_rm", 0.0, OP.is_equal)
+    tz("G8", "i_g8", 0.0, OP.is_equal)
+    tz("BM", "i_bm", 0.0, OP.is_equal)
+    tz("U1", "i_dp", -1.0, OP.is_equal)
+    tz("IDN", "i_dp", 0.0, OP.is_equal)
+    tz("LTu", "i_dp", 0.0, OP.is_ge)
+    t2("U1", "U1", "BM", OP.mult)
+    V(["G8", "COMBX"], ["COMBX"], cp(T.COMBX[:, 15:143:16], z("G8")))
+    t2("SH32", "U1", "IDN", OP.subtract)
+    t2("LTB", "LTu", "BM", OP.mult)
+    ncol = [0]
+
+    def column(terms):
+        prev, key = None, None
+        for r, wt in terms:
+            c = ncol[0]
+            ncol[0] += 1
+            out = z("COLS", c, c + 1)
+            kw = {"bias": prev} if key else {}
+            S(["RM"] + ([key] if key else []), ["col%d" % c], ac(out, RMc(r), AF.Identity, scale=float(wt), **kw))
+            prev, key = out, "col%d" % c
+        return prev, key
+
+    def make_comb(v, col, key):
+        S([key, "G8", "COMB"], ["cb%d" % v], ac(T.COMB[:, v * 144 + 15:v * 144 + 143:16], z("G8"), AF.Copy, scale=col))
+
+    def scaled(out, a, col, key):
+        S([a, key], [out], ac(z(out), z(a), AF.Copy, scale=col))
+
+    colB, kB = column([(4, 1), (9, 1)])
+    S(["AUX", kB], ["AUX"], ac(T.AUX[:, 0:2304], T.AUX[:, 0:2304], AF.Identity, bias=colB))
+    colR, kR = column([(15, 4096)])
+    S(["AUX", "RM"], ["AUX"], ac(T.AUX[:, 2304:NW], T.AUX[:, 2304:NW], AF.Identity, bias=RMc(4)))
+    S(["AUX", kR], ["AUX"], ac(T.AUX[:, 0:1], T.AUX[:, 0:1], AF.Identity, bias=colR))
+    make_comb(CF, *column([(4, -1152 - 4128), (5, 32), (6, 1)]))
+    make_comb(CA, *column([(0, 32), (1, 1), (4, -4128)]))
+    make_comb(CE, RMc(15), "RM")
+
+    b32 = 129.0 - 31.0 / 64
+    V(["cpj"], ["cpj"], ts(T.CPI[:, 384:512], T.CPI[:, 384:512], 2047, BA))
+    V(["cpk"], ["cpk"], ts(T.CPI[:, 512:544], T.CPI[:, 512:544], 511, BA))
+    V(["cpi"], ["HBa"], ts(z("HB", 128, 384), T.CPI[:, 128:384], 1.0 / 32, OP.mult, b32, OP.add))
+    V(["cpi"], ["cpl0"], ts(T.CPL[:, 0:128], T.CPI[:, 0:128], 4, SR, 31, BA))
+    V(["cpi", "cpj", "cpk"], ["cpl1"], ts(T.CPL[:, 128:544], T.CPI[:, 128:544], 31, BA))
+    V(["cpi"], ["HBb"], ts(z("HB", 0, 128), T.CPI[:, 0:128], 1.0 / 512, OP.mult, 129.0 - 511.0 / 1024, OP.add))
+    V(["cpl0", "cpl1"], ["LB"], cp(z("LB"), T.CPL[:, :]))
+    V(["cpj"], ["HBc"], ts(z("HB", 384, 512), T.CPI[:, 384:512], 1.0 / 32, OP.mult, b32, OP.add))
+    V(["cpk"], ["HBd"], ts(z("HB", 512, 544), T.CPI[:, 512:544], 1.0 / 32, OP.mult, b32 + 64.0, OP.add))
+    for j, (r, key, t, a) in enumerate(((5, "HBa", "HB", 256), (6, "LB", "LB", 256), (0, "HBb", "HB", 0), (1, "LB", "LB", 0),
+                                        (2, "HBa", "HB", 128), (3, "LB", "LB", 128), (7, "HBc", "HB", 384), (8, "LB", "LB", 384))):
+        dma("y", [key, "AUX"], ["ar%d" % j], (T.AUX[r:128:16, 0:2048], z(t, a, a + 128)))
+    dma("y", ["HBd", "AUX"], ["ar8"], (T.AUX[7:128:16, 2048:NW], z("HB", 512, 544)))
+    dma("y", ["LB", "AUX"], ["ar9"], (T.AUX[8:128:16, 2048:NW], z("LB", 512, 544)))
+    dma("y", [], ["vv1"], *[(T.VV[i:128:16, 1536:6144], T.vv[:, 1536:6144]) for i in range(16)])
+    dma("y", [], ["vv2"], *[(T.VV[i:128:16, 6144:12288], T.vv[:, 6144:12288]) for i in range(16)])
+
+    for k in range(4):
+        a, b = 512 * k, 512 * k + 512
+        V(["tab%d" % k], ["yb%d" % k], ts(T.YB[:, a:b], T.tabI[:, a:b], -7.5, OP.add, 201326592.0, OP.add))
+        V(["tab%d" % k], ["ci%d" % k], ts(T.CI[:, a:b], T.tabI[:, a:b], 15, BA))
+        S(["yb%d" % k], ["st%d" % k], ac(T.ST[:, a:b], T.YB[:, a:b], AF.Identity, bias=-12584064.0, scale=0.0625))
+        P, o = PX[k // 2], 1024 * (k % 2)
+        pk = (PK0 if k % 2 == 0 else PK2)[k // 2]
+        PE(["st%d" % k, "SH32", "cb%d" % CF] + AUXK, [pk], mm(P[:, o:o + 512], z("SH32"), T.ST[:, a:b], True, False),
+           mm(P[:, o:o + 512], comb(CF, 15), T.AUX[:, a:b], False, True))
+        S([pk], ["dt%d" % k], ac(T.DT[:, a:b], P[:, o:o + 512], AF.Copy))
+    for k in range(4):
+        a, b = 512 * k, 512 * k + 512
+        V(["ci%d" % k], ["w1%d" % k], ts(T.W1[:, a:b], T.CI[:, a:b], 1.03, OP.mult, 128.48, OP.add))
+        V(["w1%d" % k], ["wt%d" % k], ts(T.WT[:, a:b], T.W1[:, a:b], -128.0, OP.add))
+    V([], ["m0"], ms(T.MM[:, 0:H], 1.0))
+    V([], ["m1"], ms(T.MM[:, H:1536], 1.0))
+    V(["CXI"], ["c0_0", "c0_1"], cp(T.CL[:, 0:96], z("CXI")))
+    WTK = ["WT", "WTz"] + ["wt%d" % k for k in range(4)]
+    DTK = ["DT", "DTz"] + ["dt%d" % k for k in range(4)]
+    STK = ["STz"] + ["st%d" % k for k in range(4)]
+    cR, nkR = column([(15, -1)])
+    S([nkR], ["d0c"], ac(z("d0c"), cR, AF.Identity, bias=1.0))
+    S(["d0c", "dt0"], ["dt0"], ac(T.DT[:, 0:1], T.DT[:, 0:1], AF.Copy, scale=z("d0c")))
+    scaled("NI", "IDN", -1.0, "IDN")
+    scaled("LT", "LTB", 256.0, "LTB")
+    scaled("R15", "IDN", RMc(15), "RM")
+    scaled("ESC", "BM", *column([(15, -32)]))
+    V([], ["WTz"], ms(T.WT[:, 2048:NW], 0.0))
+    V([], ["DTz"], ms(T.DT[:, 2048:2304], 0.0))
+
+    def zeros():
+        dma("y", ["ZB", "VW"], ["VW"], (T.VW[:, 0:384], T.ZB[:, 0:384]))
+        dma("y", ["ZF", "SW"], ["SW"], (T.SW[:, 0:384], z("ZF", 0, 384)))
+        dma("y", ["ZB", "LW"], ["LW"], (T.LW[:, 0:1536], T.ZB[:, :]))
+
+    def late_a():
+        V([], ["HT"], ms(z("HT"), 0.0))
+        V([], ["ZB"], ms(T.ZB[:, :], 0.0))
+        V([], ["ZF"], ms(z("ZF"), 0.0))
+        dma("y", ["ZB"], ["LBA"], (T.LBA[:, :], T.ZB[:, 0:H]))
+        dma("y", ["ZF"], ["STz"], (T.ST[:, 2048:NW], z("ZF")))
+        zeros()
+        V([], ["ONES"], ms(z("ONES"), 1.0))
+        V([], ["OB"], ms(z("OB"), 0.0))
+        V([], ["CS"], ms(z("CS", 0, 8), 0.0))
+        V([], ["Z96"], ms(z("Z96"), 0.0))
+        tz("i_pc", "i_pc", 15, BA)
+        tz("TRI", "i_dp", 0.0, OP.is_le, 8192.0, OP.mult)
+        tz("U2", "i_dp", 1.0, OP.is_equal)
+        V(["OB"], ["OB"], ms(z("OB", 112, 128), 1.0))
+        V(["i_pc"], ["PC"], cp(z("PC"), z("i_pc", 0, 1)))
+        tz("WR", "i_wr", 896.0, OP.add)
+        V(["SH32"], ["SH16"], cp(z("SH16"), z("SH32")))
+        t2("U2", "U2", "BM", OP.mult)
+        t2("BID", "U2", "IDN", OP.subtract)
+
+    late, todo = {}, []
+
+    def drain(m):
+        for _ in range(min(m, len(todo))):
+            todo.pop(0)()
+
+    def later(f, *a):
+        todo.append(lambda: f(*a))
+
+    def shifted(out, a, na, c, o=0):
+        S([a, "PC"], [out], ac(z(out, o, o + na), z(a, 0, na), AF.Identity, bias=c))
+
+    def later_comb(v, terms):
+        later(lambda: make_comb(v, *column(terms)))
+
+    def key_tiles(gg):
+        for tile, kt in (("SELK", "K8"), ("NSELK", "NK8")):
+            S(["ONES", kt], [tile + str(gg)], ac(T[tile][:, 128 * gg:128 * gg + 128], z("ONES"), AF.Copy, scale=z(kt, gg, gg + 1)))
+
+    def lane_bits():
+        S(["LBA", "RM"], ["LBA"], ac(T.LBA[:, :], T.LBA[:, :], AF.Identity, bias=RMc(15)))
+        for i in range(10):
+            dma("y", ["bit%d" % i, "LBA"], ["lb%d" % i], (T.LBA[i:128:16, :], T.BIT[0:8, 1024 * i:1024 * i + H]))
+
+    def slot_combs():
+        sa = column([(i, 1 << i) for i in range(10)] + [(15, 2048)])
+        make_comb(CSA, *sa)
+        c = ncol[0]
+        ncol[0] += 1
+        S(["RM", sa[1]], ["colx"], ac(z("COLS", c, c + 1), RMc(15), AF.Identity, bias=sa[0], scale=768.0))
+        make_comb(CSB, z("COLS", c, c + 1), "colx")
+
+    LBK = ["LBA"] + ["lb%d" % i for i in range(10)]
+
+    def keep():
+        late["keep"] = column([(0, 1), (1, 1), (2, 1), (3, 1)])
+    later(shifted, "JL", "JI", 96, z("PC"))
+    later(shifted, "J2", "JL", 96, -1663.0)
+    later(shifted, "J3", "JL", 96, 384.0)
+    later(shifted, "JD", "JL", 24, 1536.0)
+    later(shifted, "JD2", "JL", 24, 3584.0)
+    for t in range(2):
+        later(shifted, "DUM%d" % t, "JL", 8, 2304.0 + 128 * t)
+        later(shifted, "DUM%d" % t, "JL", 8, 2304.0 + 128 * t, 8)
+    later(scaled, "NI2K", "IDN", -2048.0, "IDN")
+    later(lambda: scaled("CANDM", "BM", *column([(9, -1)])))
+    later_comb(CLK, [(2, 32), (3, 1), (4, -32)])
+    later_comb(CID, [(4, -1152 - 4128), (7, 32), (8, 1)])
+    for v, r in ((C0, 0), (C7, 7), (C8, 8)):
+        later(make_comb, v, RMc(r), "RM")
+    later(lambda: scaled("K8", "G8", *column([(7, 32), (8, 1)])))
+    later(scaled, "NK8", "K8", -1.0, "K8")
+    later(lane_bits)
+    later(lambda: scaled("N01", "NI", *column([(0, 1), (1, 1)])))
+    later(keep)
+    for gg in range(8):
+        later(key_tiles, gg)
+    later(slot_combs)
+    later(lambda: S(LBK, ["LBB"], ac(T.LBB[:, :], T.LBA[:, :], AF.Identity, bias=-200.0, scale=400.0)))
+
+    def lists(p, idx):
+        return T.CL[:, idx * 96 + 48 * p:idx * 96 + 48 * p + 48], "c%d_%d" % (idx, p)
+
+    def p1(p, idx):
+        off, ck = lists(p, idx)
+        P = PX[p]
+        S(AUXK + [ck], ["x%d" % p], ac(x[p][:, :], T.AUX[:, 0:2304].indirect(off), AF.Copy))
+        V(WTK + [ck, "m%d" % p], ["w%d" % p], tt(w[p][:, :], T.WT[:, 0:2304].indirect(off), T.MM[:, H * p:H * p + H], OP.mult))
+        PE(["w%d" % p, "BM"], [PK0[p]], mm(P[:, 0:512], z("BM"), w[p][:, 0:512], True, True),
+           mm(P[:, 512:768], z("BM"), w[p][:, 512:768], True, True))
+        PE(["x%d" % p, "cb%d" % CA], [LK[p]],
+           *[mm(LP[p][:, 0:48], comb(CA, i), x[p][:, i:H:16], i == 0, False) for i in range(16)])
+        S(["w%d" % p], ["n%d" % p], ac(n[p][:, :], w[p][:, :], AF.Relu, bias=-1.0))
+        PE(["x%d" % p, "n%d" % p, "R15", "LT"], [PK0[p], PK2[p]],
+           mm(P[:, 768:1024], z("R15"), x[p][:, 0:256], True, False), mm(P[:, 768:1024], z("LT"), n[p][:, 0:256], False, True),
+           mm(P[:, 1024:1536], z("R15"), x[p][:, 256:768], True, False), mm(P[:, 1024:1536], z("LT"), n[p][:, 256:768], False, True))
+
+    def p2(p, idx, k):
+        off, ck = lists(p, idx)
+        P, s = PX[p], k % SP
+        vk = "vv%d" % (0 if k == 0 else 1 if k < 4 else 2)
+        V([vk, PK0[p]], ["Y%d" % p], tt(Y[p][:, :], T.VV[:, k * 1536 + H * p:k * 1536 + H * p + H], P[:, 0:768], OP.mult))
+        V(["Y%d" % p, PK0[p], PK2[p]], ["k%d" % p], tt(cond[p][:, :], P[:, 768:1536], Y[p][:, :], OP.is_le))
+        V(DTK + [ck, "k%d" % p], ["X%d" % p], tt(X[p][:, :], T.DT[:, 0:2304].indirect(off), cond[p][:, :], OP.mult))
+
+        def esc_list():
+            if s == SP - 1:
+                PE(["k%d" % p, "cb%d" % CE], [PK2[p]],
+                   *[mm(P[:, 1024:1072], comb(CE, i), cond[p][:, i:H:16], i == 0, i == 15) for i in range(16)])
+            elif p == 0:
+                PE(["k0", "cb%d" % CE], [PK2[0]],
+                   *[mm(P[:, 1024:1032], comb(CE, i), cond[0][:, i:128:16], i == 0, i == 15) for i in range(16)])
+                S([PK2[0]], ["HT"], ac(z("HT", s + 2, 40, 5), P[:, 1024:1032], AF.Copy))
+
+        def marks():
+            if k == RO * SP - 1:
+                return
+            f = []
+            for a, b in ((0, 512), (512, 768)):
+                f += [mm(P[:, a:b], z("IDN"), T.MM[:, H * p + a:H * p + b], True, False),
+                      mm(P[:, a:b], z("NI"), w[p][:, a:b], False, False), mm(P[:, a:b], z("ESC"), cond[p][:, a:b], False, True)]
+            PE(["m%d" % p, "w%d" % p, "k%d" % p, "IDN", "NI", "ESC"], [PK0[p]], *f)
+            S([PK0[p]], ["m%d" % p], ac(T.MM[:, H * p:H * p + H], P[:, 0:768], AF.Sigmoid, bias=8064.0, scale=256.0))
+
+        def xlist():
+            PE(["X%d" % p, "COMBX"], [LK[p]],
+               *[mm(LP[p][:, 0:48], combx(i), X[p][:, i:H:16], False, i == 15) for i in range(16)])
+        for f in ((esc_list, xlist, marks) if s == SP - 1 else (marks, xlist, esc_list)):
+            f()
+
+    def v5(p, idx, rnd):
+        off, ck = lists(p, idx)
+        if rnd == 0:
+            V([LK[p]], [ck], cp(off, LP[p][:, 0:48]))
+        else:
+            t = z("CIT", 48 * p, 48 * p + 48)
+            V([LK[p]], ["cit%d" % p], cp(t, LP[p][:, 0:48]))
+            V(["cit%d" % p], ["cit%d" % p], ts(t, t, 4095, BA))
+            V(["cit%d" % p], [ck], cp(off, t))
+
+    nxt = T.cores[(rank + 1) % len(T.cores)]
+    rid, pid = topo.addr(nxt, core)
+    rmask, ne = topo.mask(core, nxt), len(topo.engines(core, nxt))
+    V([], ["DL"], ms(z("DL"), 0.0))
+
+    for rnd in range(RO):
+        base = 5 * rnd
+        for s in range(SP):
+            k, idx = rnd * SP + s, base + s
+            for p in (0, 1):
+                if s:
+                    v5(p, idx, rnd)
+                p1(p, idx)
+                drain(3 if k else 0)
+            if k == 0:
+                late_a()
+            V(["c%d_0" % idx], ["DL"], cp(z("DL", s + 1, 40, 5), T.CL[:, idx * 96:idx * 96 + 8]))
+            for p in (0, 1):
+                p2(p, idx, k)
+                drain(3)
+            if k == SP:
+                zeros()
+        drain(len(todo))
+        i4 = base + SP
+        LA, LB = T.LAp, T.LBp
+        nl = T.CL[:, i4 * 96:i4 * 96 + 8]
+        nk = "c%d_0" % i4
+        V([PK2[0]], ["E16a"], cp(z("E16", 0, 48), T.PA[:, 1024:1072]))
+        v5(0, i4, rnd)
+        V([PK2[1]], ["E16b"], cp(z("E16", 48, 96), T.PB[:, 1024:1072]))
+        v5(1, i4, rnd)
+        PE(["E16a", "E16b", "LTB", "NI2K", "BM"], ["#LA"], mm(LA[:, 128:224], z("LTB"), z("E16"), True, False),
+           mm(LA[:, 128:224], z("NI2K"), z("E16"), False, True), mm(LA[:, 256:352], z("BM"), z("E16"), True, True))
+        off, ck = lists(0, i4)
+        S(AUXK + [ck], ["A20"], ac(T.A2[:, 0:H], T.AUX[:, 0:2304].indirect(off), AF.Copy))
+        DUM = "DUM%d" % rnd
+        t2("hd", "HT", "DL", OP.mult)
+        V(["HT", "E16a"], ["CAND"], tt(z("CAND", 0, 8), z("HT", 4, 40, 5), z("E16", 0, 8), OP.is_gt),
+          tt(z("CAND", 8, 16), z("HT", 4, 40, 5), z("E16", 0, 8), OP.is_gt))
+        t2("d1", "DL", "hd", OP.subtract)
+        V(["#LA", "Z96", "CS"], ["CS1"],
+          lambda e: e.tensor_tensor_scan(z("CS", 1, 97), LA[:, 256:352], z("Z96"), 0.0, OP.add, OP.add))
+        V(["HT", "d1"], ["FS"], lambda e: e.tensor_tensor_scan(z("FS"), z("HT"), z("d1"), 0.0, OP.mult, OP.add))
+        V(["#LA", "CS", "CS1"], ["CNT"], tt(z("CNT"), LA[:, 128:224], z("CS", 0, 96), OP.add))
+        V(["FS", "DL", DUM], ["KT"], tt(z("KT", 0, 8), z("FS", 3, 40, 5), z(DUM, 0, 8), OP.subtract),
+          tt(z("KT", 8, 16), z("DL", 4, 40, 5), z(DUM, 0, 8), OP.subtract))
+        tz("OKT", "CNT", -1663.5, OP.is_le)
+        t2("TT", "CNT", "J2", OP.subtract)
+        t2("KT2", "KT", "CAND", OP.mult)
+        t2("TT2", "TT", "OKT", OP.mult)
+        t2("KK", "KT2", DUM, OP.add)
+        t2("POSF", "TT2", "J3", OP.add)
+        V(["POSF"], ["POS"], cp(z("POS"), z("POSF")))
+        V(["KK"], ["FK"], cp(z("FK"), z("KK")))
+        S(["LBB", "POS", "SW"], ["SW"], ac(T.SW[:, :].indirect(z("POS", 48, 96)), T.LBB[:, :], AF.Sigmoid))
+        V(LBK + ["POS", "VW"], ["VW"], cp(T.VW[:, :].indirect(z("POS", 0, 48)), T.LBA[:, :]))
+        off, ck = lists(1, i4)
+        V(AUXK + [ck], ["A21"], cp(T.A2[:, H:1536], T.AUX[:, 0:2304].indirect(off)))
+        S(["SW"], ["SWb"], ac(z("SWb"), T.SW[:, 0:384], AF.Copy))
+        S(AUXK + ["FK"], ["XF"], ac(z("XF"), T.AUX[:, :].indirect(z("FK")), AF.Copy))
+        PE(["VW", "SWb", "cb%d" % CSA, "cb%d" % CSB], ["#LA"],
+           *([mm(LA[:, 384:408], comb(CSA, i), T.VW[:, i:384:16], i == 0, False) for i in range(16)]
+             + [mm(LA[:, 384:408], comb(CSB, i), z("SWb", i, 384, 16), False, i == 15) for i in range(16)]))
+        SND, RCV = T["SND%d" % rnd], T["RCV%d" % rnd]
+        sk, rk = "SND%d" % rnd, "RCV%d" % rnd
+        V(["#LA"], ["LNE"], ts(z("LNE"), LA[:, 384:408], -2048.0, OP.add, 0.0, OP.max))
+        V(["#LA"], ["T1"], ts(z("T1"), LA[:, 384:408], 2047.5, OP.is_ge))
+        V(["#LA"], [sk + "b"], ts(SND[:, 384:408], LA[:, 384:408], 2047.5, OP.is_ge))
+        S(["A20", "A21", "LNE"], [sk + "a"], ac(SND[:, 0:384], T.A2[:, :].indirect(z("LNE")), AF.Copy))
+        width = 408
+        if rnd == 0:
+            V(["m0", "m1", "LNE"], [sk + "c"], cp(SND[:, 408:792], T.MM[:, 0:1536].indirect(z("LNE"))))
+            width = 792
+        do_waits("q", [sk + c for c in "abc"[:2 if rnd else 3]], [])
+        g.remote_dma(RCV[:, 0:width], SND[:, 0:width], T.sem["arr%d" % rnd], T.sem["snt%d" % rnd], pid, rid, rmask)
+        used["snt%d" % rnd] = ne
+        used["arr%d" % rnd] = ne
+        record(("rem%d" % rnd, "arr%d" % rnd, ne, {}), [], [rk])
+        V(["#LA", "JD2"], ["LNF"], tt(z("LNF"), LA[:, 384:408], z("JD2"), OP.subtract))
+        S(WTK + [nk], ["ug"], ac(z("ug"), T.WT[:, 0:2304].indirect(nl), AF.Copy))
+        t2("PRE", "LNF", "T1", OP.mult)
+
+        for h in (0, 1):
+            f = []
+            xf = z("XF", 128 * h, 128 * h + 128)
+            for gg in range(8):
+                o = PX[h][:, 128 * gg:128 * gg + 128]
+                f += [mm(o, T.SELK[:, 128 * gg:128 * gg + 128], xf, True, False),
+                      mm(o, xf, T.NSELK[:, 128 * gg:128 * gg + 128], False, False), mm(o, z("IDN"), z("TRI"), False, True)]
+            PE(["XF", "IDN", "TRI"] + [c + "SELK%d" % i for i in range(8) for c in ("", "N")], [PK0[h]], *f)
+        V(["#A0"], ["EQF"], ts(T.EQF[:, :], T.PA[:, 0:1024], 0.0, OP.is_equal))
+        S(["#B0"], ["ABD"], ac(T.ABD[:, :], T.PB[:, 0:1024], AF.Abs))
+        S(["ABD"], ["EQD"], ac(T.EQD[:, :], T.ABD[:, :], AF.Relu, bias=1.0, scale=-1.0))
+        PE(["k0", "BID"], ["#A2"], mm(T.PA[:, 1152:1280], z("BID"), cond[0][:, 0:128], True, True))
+
+        def dup(h, EQ, ek):
+            o = PX[h][:, 1024:1152]
+            PE([ek, "OB", "XF", "CANDM"], [PK2[h]],
+               *([mm(o, z("OB", 112 - 16 * gg, 240 - 16 * gg), EQ[:, 128 * gg:128 * gg + 128], gg == 0, False) for gg in range(8)]
+                 + [mm(o, z("CANDM"), z("XF", 128 * h, 128 * h + 128), False, True)]))
+
+        def winners(h):
+            P = PX[h]
+            V([PK2[h]], ["AR%d" % h], ts(z("AR", 128 * h, 128 * h + 128), P[:, 1024:1152], -0.5, OP.is_lt))
+            PE(["AR%d" % h, "cb%d" % C0], [PK2[h]],
+               *[mm(P[:, 1280:1288], comb(C0, i), z("AR", 128 * h + i, 128 * h + 128, 16), i == 0, i == 15) for i in range(16)])
+
+        def offsets(h, o1, o2, off):
+            V([PK2[h], "KT2"], [o1], tt(z(o1), PX[h][:, 1280:1288], z("KT2", 8 * h, 8 * h + 8), OP.mult))
+            V([o1, DUM], [o2], tt(z(o2), z(o1), z(DUM, 0, 8), OP.add))
+            V([o2], [off], cp(z(off), z(o2)))
+        dup(0, T.EQF, "EQF")
+        V(["#A2", "RM"], ["OH"], ts(z("OH"), T.PA[:, 1152:1280], RMc(0), OP.add))
+        winners(0)
+        V(["OH", "AR0"], ["OA"], tt(z("OA"), z("OH"), z("AR", 0, 128), OP.mult))
+        S(["OA"], ["nOA"], ac(z("nOA"), z("OA"), AF.Identity, bias=1.0, scale=-1.0))
+        scaled("OA2", "OA", 2.0, "OA")
+        offsets(0, "AO", "AO2", "OFF")
+        dup(1, T.EQD, "EQD")
+        wc = 2048 + 128 * rnd
+        tz("i_u", "ug", 0.53, OP.mult, 0.45, OP.add)
+        V(WTK + ["OFF", "nOA"], ["tg"], tt(z("tg"), T.WT[:, :].indirect(z("OFF")), z("nOA"), OP.mult))
+        winners(1)
+        pw = z("OA")
+        if rnd == 0:
+            V(STK + ["OFF", "nOA"], ["tS"], tt(z("tS"), T.ST[:, :].indirect(z("OFF")), z("nOA"), OP.mult))
+            t2("qS", "OA", "WR", OP.mult)
+            V(STK + [nk], ["Sc"], cp(z("Sc"), T.ST[:, 0:2304].indirect(nl)))
+            S(AUXK + [nk], ["XC"], ac(z("XC"), T.AUX[:, 0:2304].indirect(nl), AF.Copy))
+            o = T.PA[:, 1408:1536]
+            PE(["SH16", "tS", "qS", "XF", "cb%d" % CF], ["#A2"], mm(o, z("SH16"), z("tS"), True, False),
+               mm(o, z("SH16"), z("qS"), False, False), mm(o, comb(CF, 15), z("XF", 0, 128), False, True))
+            PE(["OA", "cb%d" % C0], ["#A0"], mm(T.PA[:, 0:128], comb(C0, 0), pw, True, False),
+               mm(T.PA[:, 0:128], comb(C0, 1), pw, False, True))
+            o = T.PB[:, 0:128]
+            PE(AUXK + ["XF", "N01", "cb%d" % C7, "cb%d" % C8], ["#B0"], mm(o, comb(C7, 0), T.AUX[:, 2048:2176], True, False),
+               mm(o, comb(C8, 1), T.AUX[:, 2048:2176], False, False), mm(o, z("N01"), z("XF", 0, 128), False, True))
+            o = T.PB[:, 1408:1536]
+            PE(["SH16", "Sc", "XC", "cb%d" % CID], ["#B2"], mm(o, z("SH16"), z("Sc"), True, False),
+               mm(o, comb(CID, 15), z("XC"), False, True))
+            S(["#A2"], ["xs"], ac(z("xs"), T.PA[:, 1408:1536], AF.Copy))
+            S(["#A0"], ["FLs"], ac(z("FLs"), T.PA[:, 0:128], AF.Copy))
+            S(["#B2"], DTK, ac(T.DT[:, 2048:2176], o, AF.Copy))
+            scaled("xt", "XC", *late["keep"])
+        V(["tg", "OA2", "OFF"], WTK, tt(T.WT[:, :].indirect(z("OFF")), z("tg"), z("OA2"), OP.add))
+        V(["OH", "AR1"], ["OBm"], tt(z("OBm"), z("OH"), z("AR", 128, 256), OP.mult))
+        scaled("OBm2", "OBm", 2.0, "OBm")
+        offsets(1, "BO", "BO2", "OFD")
+        if rnd == 0:
+            tz("i_k", "xs", 1.0 / 4096, OP.mult)
+            V(["FLs", "#B0"], ["fd"], tt(z("fd"), z("FLs"), T.PB[:, 0:128], OP.mult))
+            tz("kk", "i_k", -4096.0, OP.mult)
+        V(WTK + ["OFD", "OBm"], ["s1"], tt(z("s1"), T.WT[:, :].indirect(z("OFD")), z("OBm"), OP.add))
+        if rnd == 0:
+            V(["XF", "fd", "OFF"], AUXK, tt(T.AUX[:, :].indirect(z("OFF")), z("XF", 0, 128), z("fd"), OP.add))
+        t2("s2", "s1", "OBm2", OP.max)
+        if rnd == 0:
+            V(["kk", "xs", "OFF"], DTK, tt(T.DT[:, :].indirect(z("OFF")), z("kk"), z("xs"), OP.add))
+        tz("s3", "s2", 16.0, OP.min)
+        if rnd == 0:
+            V(["xt"] + AUXK, AUXK, tt(T.AUX[:, 2048:2176], z("xt"), T.AUX[:, 2048:2176], OP.add))
+        V(["s3", "OFD"], WTK, cp(T.WT[:, :].indirect(z("OFD")), z("s3")))
+        V(["i_u", "AR0"], WTK, tt(T.WT[:, wc:wc + 128], z("i_u"), z("AR", 0, 128), OP.mult))
+        V([nk, "c%d_1" % i4], ["CLF"], cp(z("CLF"), T.CL[:, i4 * 96:i4 * 96 + 96]))
+        if rnd == RO - 1:
+            for a, b, q in ((0, 1152, "y"), (1152, 2304, "s")):
+                V(WTK, ["yn%d" % a], ts(T.YN[:, a:b], T.WT[:, a:b], -1.0, OP.add, 0.0, OP.max))
+                dma(q, ["yn%d" % a], [], (T.yn[:, a:b], T.YN[:, a:b]))
+        V([rk, "PRE"], ["RX1"], tt(z("RX1"), RCV[:, 384:408], z("PRE"), OP.mult))
+        t2("RX2", "RX1", "JD", OP.add)
+        V(["RX2"], ["TO"], cp(z("TO"), z("RX2")))
+        V([rk, "TO", "LW"], ["LW"], cp(T.LW[:, :].indirect(z("TO")), RCV[:, 0:384]))
+        if rnd == 0:
+            V([rk, "TO", "m0", "m1"], ["m0", "m1"], cp(T.MM[:, :].indirect(z("TO")), RCV[:, 408:792]))
+        PE(["LW", "cb%d" % CLK], ["#LB"], *[mm(LB[:, 128:224], comb(CLK, i), T.LW[:, i:1536:16], i == 0, i == 15) for i in range(16)])
+        V(["#LB", "CLF"], ["cit0", "cit1"], tt(z("CIT"), LB[:, 128:224], z("CLF"), OP.max))
+        V(["cit0", "cit1"], ["cit0", "cit1"], ts(z("CIT"), z("CIT"), 4095, BA))
+        if rnd < RO - 1:
+            V(["cit0", "cit1"], ["c%d_0" % (i4 + 1), "c%d_1" % (i4 + 1)], cp(T.CL[:, (i4 + 1) * 96:(i4 + 2) * 96], z("CIT")))
+            V(["#LB"], ["HF"], ts(z("HF"), LB[:, 128:136], 4095.5, OP.is_ge))
+            V(["FS"], ["DL"], cp(z("DL", 0, 40, 5), z("FS", 4, 40, 5)))
+            V(["HF", "E16a"], ["HT"], tt(z("HT", 1, 40, 5), z("E16", 0, 8), z("HF"), OP.subtract))
+        else:
+            V(["cit0", "cit1"], ["YC"], cp(z("YC"), z("CIT")))
+            dma("y", ["YC"], [], (T.yc[:, :], z("YC")))
+
+    for q in ("v", "s", "t", "q"):
+        g.wait_ge(T.sem[q], cnt[q])
+    for name, val in used.items():
+        g.wait_ge(T.sem[name], val)

@@ -27,16 +27,16 @@ sb(I32, tabI=2048, CI=2048, CPI=544, CPL=544)
 sb(F32, YB=2048, ST=NW, DT=NW, Y0=H, Y1=H, LBB=H, SW=1920)
 sb(B16, W1=2048, WT=NW, AUX=NW, VV=12288, w0=H, w1=H, n0=H, n1=H, x0=H, x1=H, k0=H, k1=H, MM=1920, YN=2304, BIT=10240, LBA=H,
    VW=1920, A2=1536, SND0=792, SND1=792, RCV0=792, RCV1=792, LW=1920, SELK=1024, NSELK=1024, EQF=1024, EQD=1024, ABD=1024,
-   COMB=1440, ZB=1536)
+   COMB=1440, ZB=1536, FB=2048)
 sb(F16, X0=H, X1=H, COMBX=144)
 sb(U16, CL=960)
-pool("zi", I32, CXI=96, CIT=96, i_rm=16, i_pc=16, i_g8=8, i_bm=128, i_dp=128, i_wr=128, i_k=128, i_u=128)
+pool("zi", I32, CXI=96, CIT=96, i_rm=16, i_pc=16, i_g8=8, i_bm=128, i_dp=128, i_sf=128, i_wr=128, i_k=128, i_u=128)
 pool("zf", F32, RM=16, PC=1, G8=8, SH32=128, JI=96, JL=96, J2=96, J3=96, JD=24, JD2=24, DUM0=16, DUM1=16, CLF=96, YC=96, HT=40,
      DL=40, hd=40, d1=40, FS=40, KT=16, KT2=16, KK=16, CAND=16, CS=104, Z96=96, CNT=96, OKT=96, TT=96, TT2=96, POSF=96, PRE=24,
      LNF=24, T1=24, RX1=24, RX2=24, AO=8, AO2=8, BO=8, BO2=8, HF=8, xs=128, kk=128, K8=8, NK8=8, COLS=64, ZF=512, d0c=1)
 pool("zb", B16, BM=128, IDN=128, NI=128, LT=128, LTB=128, TRI=128, R15=128, ESC=128, CANDM=128, BID=128, N01=128, NI2K=128,
-     U1=128, U2=128, LTu=128, ONES=128, OB=240, SWb=384, E16=96, HB=544, LB=544, XF=256, XC=128, AR=256, OH=128, OA=128, nOA=128,
-     OA2=128, OBm=128, OBm2=128, tg=128, s1=128, s2=128, s3=128, ug=128, FLs=128, fd=128, xt=128)
+     U1=128, U2=128, LTu=128, SELF=128, SF2=128, E0=128, ID2=128, ONES=128, OB=240, SWb=384, E16=96, HB=544, LB=544, XF=256,
+     XC=128, AR=256, OA=128, nOA=128, OA2=128, OBm=128, tg=128, s1=128, s2=128, s3=128, ug=128, FLs=128, fd=128, xt=128)
 pool("zh", F16, SH16=128, WR=128, tS=128, qS=128, Sc=128)
 pool("zu", U16, POS=96, LNE=24, TO=24, FK=16, OFF=8, OFD=8)
 for nm, nc in (("PA", 1536), ("PB", 1536), ("LAp", 512), ("LBp", 512)):
@@ -161,11 +161,12 @@ def rank_program(g, core, T, topo):
     def RMc(r):
         return z("RM", r, r + 1)
 
-    dma("y", [], ["cpi"], (T.CPI[:, 256:384], T.suf[:, :]), (T.CPI[:, 0:128], T.tab[0:128:16, :]), (T.CPI[:, 128:256], T.lnk[:, :]))
+    dma("y", [], ["cpF"], (T.CPI[:, 256:384], T.suf[:, :]))
+    dma("s", [], ["cpT"], (T.CPI[:, 0:128], T.tab[0:128:16, :]))
+    dma("y", [], ["cpL"], (T.CPI[:, 128:256], T.lnk[:, :]))
     for k in range(4):
         dma("s" if k % 2 == 0 else "y", [], ["tab%d" % k], (T.tabI[:, 512 * k:512 * k + 512], T.tab[:, 512 * k:512 * k + 512]))
     dma("y", [], ["CXI"], (z("CXI"), T.cx[:, :]))
-    dma("y", [], ["vv0"], *[(T.VV[i:128:16, 0:1536], T.vv[:, 0:1536]) for i in range(16)])
 
     def iota(tile, key, pattern, base, cm, **kw):
         op("q", [], [key], lambda e: e.iota(tile, pattern, base, cm, **kw))
@@ -174,6 +175,7 @@ def rank_program(g, core, T, topo):
     iota(z("i_g8"), "i_g8", [[-16, 8]], 0, 1)
     iota(z("i_bm"), "i_bm", [[-16, 8], [0, 16]], 0, 1)
     iota(z("i_dp"), "i_dp", [[1, 128]], 0, -1)
+    iota(z("i_sf"), "i_sf", [[1, 128]], -15, -16)
     iota(T.CPI[:, 384:512], "cpj", [[1, 128]], 0, 128)
     iota(T.CPI[:, 512:544], "cpk", [[1, 32]], 0, 32)
     iota(z("i_pc"), "i_pc", [[0, 16]], 0, 1)
@@ -197,8 +199,15 @@ def rank_program(g, core, T, topo):
     tz("LTu", "i_dp", 0.0, OP.is_ge)
     t2("U1", "U1", "BM", OP.mult)
     V(["G8", "COMBX"], ["COMBX"], cp(T.COMBX[:, 15:143:16], z("G8")))
+    tz("SELF", "i_sf", 0.0, OP.is_equal, 32.0, OP.mult)
+    tz("SF2", "i_sf", -128.0, OP.is_equal)
     t2("SH32", "U1", "IDN", OP.subtract)
+    t2("SELF", "SELF", "SF2", OP.add)
     t2("LTB", "LTu", "BM", OP.mult)
+    V([], ["ONES"], ms(z("ONES"), 1.0))
+    V([], ["WTz"], ms(T.WT[:, 2048:NW], 0.0))
+    V([], ["DTz"], ms(T.DT[:, 2048:2304], 0.0))
+    V([], ["DL"], ms(z("DL"), 0.0))
     ncol = [0]
 
     def column(terms):
@@ -223,18 +232,25 @@ def rank_program(g, core, T, topo):
     colR, kR = column([(15, 4096)])
     S(["AUX", "RM"], ["AUX"], ac(T.AUX[:, 2304:NW], T.AUX[:, 2304:NW], AF.Identity, bias=RMc(4)))
     S(["AUX", kR], ["AUX"], ac(T.AUX[:, 0:1], T.AUX[:, 0:1], AF.Identity, bias=colR))
+    colF, kF = column([(15, -1152 - 4128)])
     make_comb(CF, *column([(4, -1152 - 4128), (5, 32), (6, 1)]))
     make_comb(CA, *column([(0, 32), (1, 1), (4, -4128)]))
     make_comb(CE, RMc(15), "RM")
+    scaled("NI", "IDN", -1.0, "IDN")
+    scaled("LT", "LTB", 256.0, "LTB")
+    scaled("R15", "IDN", RMc(15), "RM")
+    scaled("ESC", "BM", *column([(15, -32)]))
 
     b32 = 129.0 - 31.0 / 64
     V(["cpj"], ["cpj"], ts(T.CPI[:, 384:512], T.CPI[:, 384:512], 2047, BA))
     V(["cpk"], ["cpk"], ts(T.CPI[:, 512:544], T.CPI[:, 512:544], 511, BA))
-    V(["cpi"], ["HBa"], ts(z("HB", 128, 384), T.CPI[:, 128:384], 1.0 / 32, OP.mult, b32, OP.add))
-    V(["cpi"], ["cpl0"], ts(T.CPL[:, 0:128], T.CPI[:, 0:128], 4, SR, 31, BA))
-    V(["cpi", "cpj", "cpk"], ["cpl1"], ts(T.CPL[:, 128:544], T.CPI[:, 128:544], 31, BA))
-    V(["cpi"], ["HBb"], ts(z("HB", 0, 128), T.CPI[:, 0:128], 1.0 / 512, OP.mult, 129.0 - 511.0 / 1024, OP.add))
+    V(["cpF", "cpL"], ["HBa"], ts(z("HB", 128, 384), T.CPI[:, 128:384], 1.0 / 32, OP.mult, b32, OP.add))
+    V(["cpT"], ["cpl0"], ts(T.CPL[:, 0:128], T.CPI[:, 0:128], 4, SR, 31, BA))
+    V(["cpF", "cpL", "cpj", "cpk"], ["cpl1"], ts(T.CPL[:, 128:544], T.CPI[:, 128:544], 31, BA))
+    V(["cpT"], ["HBb"], ts(z("HB", 0, 128), T.CPI[:, 0:128], 1.0 / 512, OP.mult, 129.0 - 511.0 / 1024, OP.add))
     V(["cpl0", "cpl1"], ["LB"], cp(z("LB"), T.CPL[:, :]))
+    dma("y", ["HBa"], ["fb0"], (T.FB[0:8, :], z("HB", 256, 384)))
+    dma("y", ["LB"], ["fb1"], (T.FB[8:16, :], z("LB", 256, 384)))
     V(["cpj"], ["HBc"], ts(z("HB", 384, 512), T.CPI[:, 384:512], 1.0 / 32, OP.mult, b32, OP.add))
     V(["cpk"], ["HBd"], ts(z("HB", 512, 544), T.CPI[:, 512:544], 1.0 / 32, OP.mult, b32 + 64.0, OP.add))
     for j, (r, key, t, a) in enumerate(((5, "HBa", "HB", 256), (6, "LB", "LB", 256), (0, "HBb", "HB", 0), (1, "LB", "LB", 0),
@@ -242,25 +258,23 @@ def rank_program(g, core, T, topo):
         dma("y", [key, "AUX"], ["ar%d" % j], (T.AUX[r:128:16, 0:2048], z(t, a, a + 128)))
     dma("y", ["HBd", "AUX"], ["ar8"], (T.AUX[7:128:16, 2048:NW], z("HB", 512, 544)))
     dma("y", ["LB", "AUX"], ["ar9"], (T.AUX[8:128:16, 2048:NW], z("LB", 512, 544)))
-    dma("y", [], ["vv1"], *[(T.VV[i:128:16, 1536:6144], T.vv[:, 1536:6144]) for i in range(16)])
-    dma("y", [], ["vv2"], *[(T.VV[i:128:16, 6144:12288], T.vv[:, 6144:12288]) for i in range(16)])
+    for key, a, b in (("vv0", 0, 1536), ("vv1", 1536, 6144), ("vv2", 6144, 12288)):
+        dma("y", [], [key], *[(T.VV[i:128:16, a:b], T.vv[:, a:b]) for i in range(16)])
 
     for k in range(4):
         a, b = 512 * k, 512 * k + 512
         V(["tab%d" % k], ["yb%d" % k], ts(T.YB[:, a:b], T.tabI[:, a:b], -7.5, OP.add, 201326592.0, OP.add))
         V(["tab%d" % k], ["ci%d" % k], ts(T.CI[:, a:b], T.tabI[:, a:b], 15, BA))
         S(["yb%d" % k], ["st%d" % k], ac(T.ST[:, a:b], T.YB[:, a:b], AF.Identity, bias=-12584064.0, scale=0.0625))
-        P, o = PX[k // 2], 1024 * (k % 2)
-        pk = (PK0 if k % 2 == 0 else PK2)[k // 2]
-        PE(["st%d" % k, "SH32", "cb%d" % CF] + AUXK, [pk], mm(P[:, o:o + 512], z("SH32"), T.ST[:, a:b], True, False),
-           mm(P[:, o:o + 512], comb(CF, 15), T.AUX[:, a:b], False, True))
-        S([pk], ["dt%d" % k], ac(T.DT[:, a:b], P[:, o:o + 512], AF.Copy))
-    for k in range(4):
-        a, b = 512 * k, 512 * k + 512
-        V(["ci%d" % k], ["w1%d" % k], ts(T.W1[:, a:b], T.CI[:, a:b], 1.03, OP.mult, 128.48, OP.add))
-        V(["w1%d" % k], ["wt%d" % k], ts(T.WT[:, a:b], T.W1[:, a:b], -128.0, OP.add))
-    V([], ["m0"], ms(T.MM[:, 0:H], 1.0))
-    V([], ["m1"], ms(T.MM[:, H:1536], 1.0))
+    pieces = [(k, 512 * k, PX[k // 2][:, 1024 * (k % 2):1024 * (k % 2) + 512], (PK0 if k % 2 == 0 else PK2)[k // 2]) for k in range(4)]
+    o = WHERE["SELF"][1]
+    for k, a, P, pk in pieces:
+        PE(["st%d" % k, "SH32", "SELF", "fb0", "fb1"], [pk], mm(P, z("SH32"), T.ST[:, a:a + 512], True, False),
+           mm(P, T.zb[0:16, o:o + 128], T.FB[0:16, a:a + 512], False, True))
+        V(["ci%d" % k], ["w1%d" % k], ts(T.W1[:, a:a + 512], T.CI[:, a:a + 512], 1.03, OP.mult, 128.48, OP.add))
+        V(["w1%d" % k], ["wt%d" % k], ts(T.WT[:, a:a + 512], T.W1[:, a:a + 512], -128.0, OP.add))
+    for k, a, P, pk in pieces:
+        S([pk, kF], ["dt%d" % k], ac(T.DT[:, a:a + 512], P, AF.Identity, bias=colF))
     V(["CXI"], ["c0_0", "c0_1"], cp(T.CL[:, 0:96], z("CXI")))
     WTK = ["WT", "WTz"] + ["wt%d" % k for k in range(4)]
     DTK = ["DT", "DTz"] + ["dt%d" % k for k in range(4)]
@@ -268,12 +282,6 @@ def rank_program(g, core, T, topo):
     cR, nkR = column([(15, -1)])
     S([nkR], ["d0c"], ac(z("d0c"), cR, AF.Identity, bias=1.0))
     S(["d0c", "dt0"], ["dt0"], ac(T.DT[:, 0:1], T.DT[:, 0:1], AF.Copy, scale=z("d0c")))
-    scaled("NI", "IDN", -1.0, "IDN")
-    scaled("LT", "LTB", 256.0, "LTB")
-    scaled("R15", "IDN", RMc(15), "RM")
-    scaled("ESC", "BM", *column([(15, -32)]))
-    V([], ["WTz"], ms(T.WT[:, 2048:NW], 0.0))
-    V([], ["DTz"], ms(T.DT[:, 2048:2304], 0.0))
 
     def zeros():
         dma("y", ["ZB", "VW"], ["VW"], (T.VW[:, 0:384], T.ZB[:, 0:384]))
@@ -287,7 +295,6 @@ def rank_program(g, core, T, topo):
         dma("y", ["ZB"], ["LBA"], (T.LBA[:, :], T.ZB[:, 0:H]))
         dma("y", ["ZF"], ["STz"], (T.ST[:, 2048:NW], z("ZF")))
         zeros()
-        V([], ["ONES"], ms(z("ONES"), 1.0))
         V([], ["OB"], ms(z("OB"), 0.0))
         V([], ["CS"], ms(z("CS", 0, 8), 0.0))
         V([], ["Z96"], ms(z("Z96"), 0.0))
@@ -345,6 +352,8 @@ def rank_program(g, core, T, topo):
     for t in range(2):
         later(shifted, "DUM%d" % t, "JL", 8, 2304.0 + 128 * t)
         later(shifted, "DUM%d" % t, "JL", 8, 2304.0 + 128 * t, 8)
+    later(scaled, "E0", "IDN", RMc(0), "RM")
+    later(scaled, "ID2", "IDN", 2.0, "IDN")
     later(scaled, "NI2K", "IDN", -2048.0, "IDN")
     later(lambda: scaled("CANDM", "BM", *column([(9, -1)])))
     later_comb(CLK, [(2, 32), (3, 1), (4, -32)])
@@ -364,11 +373,13 @@ def rank_program(g, core, T, topo):
     def lists(p, idx):
         return T.CL[:, idx * 96 + 48 * p:idx * 96 + 48 * p + 48], "c%d_%d" % (idx, p)
 
-    def p1(p, idx):
+    def p1(p, idx, k):
         off, ck = lists(p, idx)
         P = PX[p]
         S(AUXK + [ck], ["x%d" % p], ac(x[p][:, :], T.AUX[:, 0:2304].indirect(off), AF.Copy))
-        V(WTK + [ck, "m%d" % p], ["w%d" % p], tt(w[p][:, :], T.WT[:, 0:2304].indirect(off), T.MM[:, H * p:H * p + H], OP.mult))
+        wi = T.WT[:, 0:2304].indirect(off)
+        V(WTK + [ck] + (["m%d" % p] if k else []), ["w%d" % p],
+          tt(w[p][:, :], wi, T.MM[:, H * p:H * p + H], OP.mult) if k else cp(w[p][:, :], wi))
         PE(["w%d" % p, "BM"], [PK0[p]], mm(P[:, 0:512], z("BM"), w[p][:, 0:512], True, True),
            mm(P[:, 512:768], z("BM"), w[p][:, 512:768], True, True))
         PE(["x%d" % p, "cb%d" % CA], [LK[p]],
@@ -400,16 +411,24 @@ def rank_program(g, core, T, topo):
                 return
             f = []
             for a, b in ((0, 512), (512, 768)):
-                f += [mm(P[:, a:b], z("IDN"), T.MM[:, H * p + a:H * p + b], True, False),
-                      mm(P[:, a:b], z("NI"), w[p][:, a:b], False, False), mm(P[:, a:b], z("ESC"), cond[p][:, a:b], False, True)]
-            PE(["m%d" % p, "w%d" % p, "k%d" % p, "IDN", "NI", "ESC"], [PK0[p]], *f)
-            S([PK0[p]], ["m%d" % p], ac(T.MM[:, H * p:H * p + H], P[:, 0:768], AF.Sigmoid, bias=8064.0, scale=256.0))
+                if k:
+                    f.append(mm(P[:, a:b], z("IDN"), T.MM[:, H * p + a:H * p + b], True, False))
+                f += [mm(P[:, a:b], z("NI"), w[p][:, a:b], k == 0, False), mm(P[:, a:b], z("ESC"), cond[p][:, a:b], False, True)]
+            PE(["w%d" % p, "k%d" % p, "IDN", "NI", "ESC"] + (["m%d" % p] if k else []), [PK0[p]], *f)
+            S([PK0[p]], ["m%d" % p],
+              ac(T.MM[:, H * p:H * p + H], P[:, 0:768], AF.Sigmoid, bias=8064.0 if k else 8320.0, scale=256.0))
 
         def xlist():
             PE(["X%d" % p, "COMBX"], [LK[p]],
                *[mm(LP[p][:, 0:48], combx(i), X[p][:, i:H:16], False, i == 15) for i in range(16)])
-        for f in ((esc_list, xlist, marks) if s == SP - 1 else (marks, xlist, esc_list)):
-            f()
+        if s < SP - 1:
+            marks()
+            xlist()
+            esc_list()
+            return None
+        esc_list()
+        xlist()
+        return marks
 
     def v5(p, idx, rnd):
         off, ck = lists(p, idx)
@@ -424,7 +443,6 @@ def rank_program(g, core, T, topo):
     nxt = T.cores[(rank + 1) % len(T.cores)]
     rid, pid = topo.addr(nxt, core)
     rmask, ne = topo.mask(core, nxt), len(topo.engines(core, nxt))
-    V([], ["DL"], ms(z("DL"), 0.0))
 
     for rnd in range(RO):
         base = 5 * rnd
@@ -433,14 +451,16 @@ def rank_program(g, core, T, topo):
             for p in (0, 1):
                 if s:
                     v5(p, idx, rnd)
-                p1(p, idx)
-                drain(3 if k else 0)
+                p1(p, idx, k)
+                drain(7 if k and p else 0)
             if k == 0:
                 late_a()
             V(["c%d_0" % idx], ["DL"], cp(z("DL", s + 1, 40, 5), T.CL[:, idx * 96:idx * 96 + 8]))
             for p in (0, 1):
-                p2(p, idx, k)
-                drain(3)
+                mk = p2(p, idx, k)
+                if mk and p == 0:
+                    mk()
+                drain(4 if p == 0 else 0)
             if k == SP:
                 zeros()
         drain(len(todo))
@@ -456,6 +476,9 @@ def rank_program(g, core, T, topo):
            mm(LA[:, 128:224], z("NI2K"), z("E16"), False, True), mm(LA[:, 256:352], z("BM"), z("E16"), True, True))
         off, ck = lists(0, i4)
         S(AUXK + [ck], ["A20"], ac(T.A2[:, 0:H], T.AUX[:, 0:2304].indirect(off), AF.Copy))
+        mk()
+        off, ck = lists(1, i4)
+        S(AUXK + [ck], ["A21"], ac(T.A2[:, H:1536], T.AUX[:, 0:2304].indirect(off), AF.Copy))
         DUM = "DUM%d" % rnd
         t2("hd", "HT", "DL", OP.mult)
         V(["HT", "E16a"], ["CAND"], tt(z("CAND", 0, 8), z("HT", 4, 40, 5), z("E16", 0, 8), OP.is_gt),
@@ -463,27 +486,26 @@ def rank_program(g, core, T, topo):
         t2("d1", "DL", "hd", OP.subtract)
         V(["#LA", "Z96", "CS"], ["CS1"],
           lambda e: e.tensor_tensor_scan(z("CS", 1, 97), LA[:, 256:352], z("Z96"), 0.0, OP.add, OP.add))
-        V(["HT", "d1"], ["FS"], lambda e: e.tensor_tensor_scan(z("FS"), z("HT"), z("d1"), 0.0, OP.mult, OP.add))
         V(["#LA", "CS", "CS1"], ["CNT"], tt(z("CNT"), LA[:, 128:224], z("CS", 0, 96), OP.add))
-        V(["FS", "DL", DUM], ["KT"], tt(z("KT", 0, 8), z("FS", 3, 40, 5), z(DUM, 0, 8), OP.subtract),
-          tt(z("KT", 8, 16), z("DL", 4, 40, 5), z(DUM, 0, 8), OP.subtract))
         tz("OKT", "CNT", -1663.5, OP.is_le)
         t2("TT", "CNT", "J2", OP.subtract)
-        t2("KT2", "KT", "CAND", OP.mult)
         t2("TT2", "TT", "OKT", OP.mult)
-        t2("KK", "KT2", DUM, OP.add)
         t2("POSF", "TT2", "J3", OP.add)
         V(["POSF"], ["POS"], cp(z("POS"), z("POSF")))
-        V(["KK"], ["FK"], cp(z("FK"), z("KK")))
         S(["LBB", "POS", "SW"], ["SW"], ac(T.SW[:, :].indirect(z("POS", 48, 96)), T.LBB[:, :], AF.Sigmoid))
         V(LBK + ["POS", "VW"], ["VW"], cp(T.VW[:, :].indirect(z("POS", 0, 48)), T.LBA[:, :]))
-        off, ck = lists(1, i4)
-        V(AUXK + [ck], ["A21"], cp(T.A2[:, H:1536], T.AUX[:, 0:2304].indirect(off)))
+        PE(["VW", "cb%d" % CSA], ["#LA"],
+           *[mm(LA[:, 384:408], comb(CSA, i), T.VW[:, i:384:16], i == 0, False) for i in range(16)])
         S(["SW"], ["SWb"], ac(z("SWb"), T.SW[:, 0:384], AF.Copy))
+        PE(["SWb", "cb%d" % CSB], ["#LA"],
+           *[mm(LA[:, 384:408], comb(CSB, i), z("SWb", i, 384, 16), False, i == 15) for i in range(16)])
+        V(["HT", "d1"], ["FS"], lambda e: e.tensor_tensor_scan(z("FS"), z("HT"), z("d1"), 0.0, OP.mult, OP.add))
+        V(["FS", "DL", DUM], ["KT"], tt(z("KT", 0, 8), z("FS", 3, 40, 5), z(DUM, 0, 8), OP.subtract),
+          tt(z("KT", 8, 16), z("DL", 4, 40, 5), z(DUM, 0, 8), OP.subtract))
+        t2("KT2", "KT", "CAND", OP.mult)
+        t2("KK", "KT2", DUM, OP.add)
+        V(["KK"], ["FK"], cp(z("FK"), z("KK")))
         S(AUXK + ["FK"], ["XF"], ac(z("XF"), T.AUX[:, :].indirect(z("FK")), AF.Copy))
-        PE(["VW", "SWb", "cb%d" % CSA, "cb%d" % CSB], ["#LA"],
-           *([mm(LA[:, 384:408], comb(CSA, i), T.VW[:, i:384:16], i == 0, False) for i in range(16)]
-             + [mm(LA[:, 384:408], comb(CSB, i), z("SWb", i, 384, 16), False, i == 15) for i in range(16)]))
         SND, RCV = T["SND%d" % rnd], T["RCV%d" % rnd]
         sk, rk = "SND%d" % rnd, "RCV%d" % rnd
         V(["#LA"], ["LNE"], ts(z("LNE"), LA[:, 384:408], -2048.0, OP.add, 0.0, OP.max))
@@ -514,7 +536,8 @@ def rank_program(g, core, T, topo):
         V(["#A0"], ["EQF"], ts(T.EQF[:, :], T.PA[:, 0:1024], 0.0, OP.is_equal))
         S(["#B0"], ["ABD"], ac(T.ABD[:, :], T.PB[:, 0:1024], AF.Abs))
         S(["ABD"], ["EQD"], ac(T.EQD[:, :], T.ABD[:, :], AF.Relu, bias=1.0, scale=-1.0))
-        PE(["k0", "BID"], ["#A2"], mm(T.PA[:, 1152:1280], z("BID"), cond[0][:, 0:128], True, True))
+        oh = LB[:, 256:384]
+        PE(["k0", "BID", "E0", "ONES"], ["#LB"], mm(oh, z("BID"), cond[0][:, 0:128], True, False), mm(oh, z("E0"), z("ONES"), False, True))
 
         def dup(h, EQ, ek):
             o = PX[h][:, 1024:1152]
@@ -533,9 +556,8 @@ def rank_program(g, core, T, topo):
             V([o1, DUM], [o2], tt(z(o2), z(o1), z(DUM, 0, 8), OP.add))
             V([o2], [off], cp(z(off), z(o2)))
         dup(0, T.EQF, "EQF")
-        V(["#A2", "RM"], ["OH"], ts(z("OH"), T.PA[:, 1152:1280], RMc(0), OP.add))
         winners(0)
-        V(["OH", "AR0"], ["OA"], tt(z("OA"), z("OH"), z("AR", 0, 128), OP.mult))
+        V(["#LB", "AR0"], ["OA"], tt(z("OA"), oh, z("AR", 0, 128), OP.mult))
         S(["OA"], ["nOA"], ac(z("nOA"), z("OA"), AF.Identity, bias=1.0, scale=-1.0))
         scaled("OA2", "OA", 2.0, "OA")
         offsets(0, "AO", "AO2", "OFF")
@@ -544,7 +566,6 @@ def rank_program(g, core, T, topo):
         tz("i_u", "ug", 0.53, OP.mult, 0.45, OP.add)
         V(WTK + ["OFF", "nOA"], ["tg"], tt(z("tg"), T.WT[:, :].indirect(z("OFF")), z("nOA"), OP.mult))
         winners(1)
-        pw = z("OA")
         if rnd == 0:
             V(STK + ["OFF", "nOA"], ["tS"], tt(z("tS"), T.ST[:, :].indirect(z("OFF")), z("nOA"), OP.mult))
             t2("qS", "OA", "WR", OP.mult)
@@ -553,8 +574,8 @@ def rank_program(g, core, T, topo):
             o = T.PA[:, 1408:1536]
             PE(["SH16", "tS", "qS", "XF", "cb%d" % CF], ["#A2"], mm(o, z("SH16"), z("tS"), True, False),
                mm(o, z("SH16"), z("qS"), False, False), mm(o, comb(CF, 15), z("XF", 0, 128), False, True))
-            PE(["OA", "cb%d" % C0], ["#A0"], mm(T.PA[:, 0:128], comb(C0, 0), pw, True, False),
-               mm(T.PA[:, 0:128], comb(C0, 1), pw, False, True))
+            PE(["OA", "cb%d" % C0], ["#A0"], mm(T.PA[:, 0:128], comb(C0, 0), z("OA"), True, False),
+               mm(T.PA[:, 0:128], comb(C0, 1), z("OA"), False, True))
             o = T.PB[:, 0:128]
             PE(AUXK + ["XF", "N01", "cb%d" % C7, "cb%d" % C8], ["#B0"], mm(o, comb(C7, 0), T.AUX[:, 2048:2176], True, False),
                mm(o, comb(C8, 1), T.AUX[:, 2048:2176], False, False), mm(o, z("N01"), z("XF", 0, 128), False, True))
@@ -566,8 +587,8 @@ def rank_program(g, core, T, topo):
             S(["#B2"], DTK, ac(T.DT[:, 2048:2176], o, AF.Copy))
             scaled("xt", "XC", *late["keep"])
         V(["tg", "OA2", "OFF"], WTK, tt(T.WT[:, :].indirect(z("OFF")), z("tg"), z("OA2"), OP.add))
-        V(["OH", "AR1"], ["OBm"], tt(z("OBm"), z("OH"), z("AR", 128, 256), OP.mult))
-        scaled("OBm2", "OBm", 2.0, "OBm")
+        V(["#LB", "AR1"], ["OBm"], tt(z("OBm"), oh, z("AR", 128, 256), OP.mult))
+        PE(["OBm", "ID2"], ["#LA"], mm(LA[:, 256:384], z("ID2"), z("OBm"), True, True))
         offsets(1, "BO", "BO2", "OFD")
         if rnd == 0:
             tz("i_k", "xs", 1.0 / 4096, OP.mult)
@@ -576,7 +597,7 @@ def rank_program(g, core, T, topo):
         V(WTK + ["OFD", "OBm"], ["s1"], tt(z("s1"), T.WT[:, :].indirect(z("OFD")), z("OBm"), OP.add))
         if rnd == 0:
             V(["XF", "fd", "OFF"], AUXK, tt(T.AUX[:, :].indirect(z("OFF")), z("XF", 0, 128), z("fd"), OP.add))
-        t2("s2", "s1", "OBm2", OP.max)
+        V(["s1", "#LA"], ["s2"], tt(z("s2"), z("s1"), LA[:, 256:384], OP.max))
         if rnd == 0:
             V(["kk", "xs", "OFF"], DTK, tt(T.DT[:, :].indirect(z("OFF")), z("kk"), z("xs"), OP.add))
         tz("s3", "s2", 16.0, OP.min)
@@ -585,17 +606,21 @@ def rank_program(g, core, T, topo):
         V(["s3", "OFD"], WTK, cp(T.WT[:, :].indirect(z("OFD")), z("s3")))
         V(["i_u", "AR0"], WTK, tt(T.WT[:, wc:wc + 128], z("i_u"), z("AR", 0, 128), OP.mult))
         V([nk, "c%d_1" % i4], ["CLF"], cp(z("CLF"), T.CL[:, i4 * 96:i4 * 96 + 96]))
+
+        def counts_out(a, b, q):
+            V(WTK, ["yn%d" % a], ts(T.YN[:, a:b], T.WT[:, a:b], -1.0, OP.add, 0.0, OP.max))
+            dma(q, ["yn%d" % a], [], (T.yn[:, a:b], T.YN[:, a:b]))
         if rnd == RO - 1:
-            for a, b, q in ((0, 1152, "y"), (1152, 2304, "s")):
-                V(WTK, ["yn%d" % a], ts(T.YN[:, a:b], T.WT[:, a:b], -1.0, OP.add, 0.0, OP.max))
-                dma(q, ["yn%d" % a], [], (T.yn[:, a:b], T.YN[:, a:b]))
+            counts_out(0, 1152, "s")
         V([rk, "PRE"], ["RX1"], tt(z("RX1"), RCV[:, 384:408], z("PRE"), OP.mult))
         t2("RX2", "RX1", "JD", OP.add)
         V(["RX2"], ["TO"], cp(z("TO"), z("RX2")))
         V([rk, "TO", "LW"], ["LW"], cp(T.LW[:, :].indirect(z("TO")), RCV[:, 0:384]))
+        PE(["LW", "cb%d" % CLK], ["#LB"], *[mm(LB[:, 128:224], comb(CLK, i), T.LW[:, i:1536:16], i == 0, i == 15) for i in range(16)])
         if rnd == 0:
             V([rk, "TO", "m0", "m1"], ["m0", "m1"], cp(T.MM[:, :].indirect(z("TO")), RCV[:, 408:792]))
-        PE(["LW", "cb%d" % CLK], ["#LB"], *[mm(LB[:, 128:224], comb(CLK, i), T.LW[:, i:1536:16], i == 0, i == 15) for i in range(16)])
+        else:
+            counts_out(1152, 2304, "s")
         V(["#LB", "CLF"], ["cit0", "cit1"], tt(z("CIT"), LB[:, 128:224], z("CLF"), OP.max))
         V(["cit0", "cit1"], ["cit0", "cit1"], ts(z("CIT"), z("CIT"), 4095, BA))
         if rnd < RO - 1:

from concourse.mybir import AluOpType, ActivationFunctionType

OP = AluOpType
AF = ActivationFunctionType
RO, SP = 2, 4
NW = 2560
H = 768
F32, B16, I32, F16, U16 = "float32", "bfloat16", "int32", "float16", "uint16"
SCRATCH = {}
WHERE = {}


def sb(dtype, **kw):
    for name, n in kw.items():
        SCRATCH[name] = ("sbuf", [128, n], dtype)


def pool(buf, dtype, **kw):
    o = 0
    for name, n in kw.items():
        WHERE[name] = (buf, o, n)
        o += -(-n // 16) * 16
    SCRATCH[buf] = ("sbuf", [128, o], dtype)


sb(I32, tabI=2048, CI=2048, CPI=544, CPL=544)
sb(F32, YB=2048, ST=NW, DT=NW, Y0=H, Y1=H, LBB=H, SW=1920)
sb(B16, W1=2048, WT=NW, AUX=NW, VV=12288, w0=H, w1=H, n0=H, n1=H, x0=H, x1=H, k0=H, k1=H, MM=1920, YN=2304, BIT=10240, LBA=H,
   VW=1920, A2=1536, SND0=792, SND1=792, RCV0=792, RCV1=792, LW=1920, SELK=1024, NSELK=1024, EQF=1024, EQD=1024, ABD=1024,
   COMB=1440, ZB=1536, FB=2048)
sb(F16, X0=H, X1=H, COMBX=144)
sb(U16, CL=960)
pool("zi", I32, CXI=96, CIT=96, i_rm=16, i_pc=16, i_g8=8, i_bm=128, i_dp=128, i_sf=128, i_wr=128, i_k=128, i_u=128)
pool("zf", F32, RM=16, PC=1, G8=8, SH32=128, JI=96, JL=96, J2=96, J3=96, JD=24, JD2=24, DUM0=16, DUM1=16, CLF=96, YC=96, HT=40,
     DL=40, hd=40, d1=40, FS=40, KT=16, KT2=16, KK=16, CAND=16, CS=104, Z96=96, CNT=96, OKT=96, TT=96, TT2=96, POSF=96, PRE=24,
     LNF=24, T1=24, RX1=24, RX2=24, AO=8, AO2=8, BO=8, BO2=8, HF=8, xs=128, kk=128, K8=8, NK8=8, COLS=64, ZF=512, d0c=1)
pool("zb", B16, BM=128, IDN=128, NI=128, LT=128, LTB=128, TRI=128, R15=128, ESC=128, CANDM=128, BID=128, N01=128, NI2K=128,
     U1=128, U2=128, LTu=128, SELF=128, SF2=128, E0=128, ID2=128, ONES=128, OB=240, SWb=384, E16=96, HB=544, LB=544, XF=256,
     XC=128, AR=256, OA=128, nOA=128, OA2=128, OBm=128, tg=128, s1=128, s2=128, s3=128, ug=128, FLs=128, fd=128, xt=128)
pool("zh", F16, SH16=128, WR=128, tS=128, qS=128, Sc=128)
pool("zu", U16, POS=96, LNE=24, TO=24, FK=16, OFF=8, OFD=8)
for nm, nc in (("PA", 1536), ("PB", 1536), ("LAp", 512), ("LBp", 512)):
    SCRATCH[nm] = ("psum", [128, nc], F32)

SEMAPHORES = ["v", "s", "t", "q", "arr0", "arr1", "snt0", "snt1"] + ["d%d" % i for i in range(60)]
CA, CE, CF, CID, CSA, CSB, CLK, C0, C7, C8 = range(10)


def rank_program(g, core, T, topo):
    rank = T.rank_of(core)
    if rank is None:
        return
    Q = {"v": g.vector, "s": g.scalar, "t": g.tensor, "q": g, "y": g.sync}
    cnt = {"v": 0, "s": 0, "t": 0, "q": 0}
    know = {q: {} for q in Q}
    res, acc, used, nd = {}, {}, {}, [0]

    def do_waits(q, R, W):
        deps = []
        for k in R:
            if k[0] != "#":
                deps += res.get(k, ([], []))[0]
        for k in W:
            if k[0] != "#":
                ws, rs = res.get(k, ([], []))
                deps += ws + [e for e in rs if e[0] != q]
        for k in list(R) + list(W):
            if k[0] == "#":
                deps += [e for e in acc.get(k, []) if e[0] != q]
        best = {}
        for e in deps:
            if know[q].get(e[1], 0) < e[2] and (e[1] not in best or best[e[1]][2] < e[2]):
                best[e[1]] = e
        for e in [e for e in best.values() if not any(o is not e and o[3].get(e[1], 0) >= e[2] for o in best.values())]:
            Q[q].wait_ge(T.sem[e[1]], e[2])
            k = know[q]
            k[e[1]] = max(k.get(e[1], 0), e[2])
            for s, v in e[3].items():
                k[s] = max(k.get(s, 0), v)

    def record(ent, R, W):
        for k in W:
            if k[0] != "#":
                res[k] = ([ent], [])
        for k in R:
            if k[0] != "#" and k not in W:
                ws, rs = res.get(k, ([], []))
                res[k] = (ws, [e for e in rs if e[0] != ent[0]] + [ent])
        for k in list(R) + list(W):
            if k[0] == "#":
                acc[k] = [ent]

    def op(q, R, W, *fns):
        do_waits(q, R, W)
        for fn in fns:
            fn(Q[q]).then_inc(T.sem[q], 1)
            cnt[q] += 1
        clock = dict(know[q])
        clock[q] = cnt[q]
        record((q, q, cnt[q], clock), R, W)

    def dma(q, R, W, *pairs):
        do_waits(q, R, W)
        name = "d%d" % nd[0]
        nd[0] += 1
        for o, i in pairs:
            Q[q].dma_start(o, i).then_inc(T.sem[name], 16)
        used[name] = 16 * len(pairs)
        record((name, name, 16 * len(pairs), dict(know[q])), R, W)

    def z(name, a=0, b=None, st=1):
        buf, o, n = WHERE[name]
        return T[buf][:, o + a:o + (n if b is None else b):st]

    def ts(out, a, s1, o1, s2=None, o2=None):
        if o2 is None:
            return lambda e: e.tensor_scalar(out, a, s1, None, o1)
        return lambda e: e.tensor_scalar(out, a, s1, s2, o1, o2)

    def tt(out, a, b, o):
        return lambda e: e.tensor_tensor(out, a, b, o)

    def cp(out, a):
        return lambda e: e.tensor_copy(out, a)

    def ms(out, c):
        return lambda e: e.memset(out, c)

    def ac(out, a, f, **kw):
        return lambda e: e.activation(out, a, f, **kw)

    def mm(out, l, r, st, sp):
        return lambda e: e.matmul(out, l, r, st, sp)

    def V(R, W, *f):
        op("v", R, W, *f)

    def S(R, W, *f):
        op("s", R, W, *f)

    def PE(R, W, *f):
        op("t", R, W, *f)

    def tz(out, a, s1, o1, *more):
        V([a], [out], ts(z(out), z(a), s1, o1, *more))

    def t2(out, a, b, o):
        V([a, b], [out], tt(z(out), z(a), z(b), o))

    PX, LP = [T.PA, T.PB], [T.LAp, T.LBp]
    PK0, PK2, LK = ["#A0", "#B0"], ["#A2", "#B2"], ["#LA", "#LB"]
    w, n, x, cond, X, Y = ([T["%s%d" % (a, p)] for p in (0, 1)] for a in ("w", "n", "x", "k", "X", "Y"))
    AUXK = ["AUX"] + ["ar%d" % i for i in range(10)]

    def comb(v, i):
        return T.COMB[:, v * 144 + 15 - i:v * 144 + 143 - i]

    def combx(i):
        return T.COMBX[:, 15 - i:143 - i]

    def RMc(r):
        return z("RM", r, r + 1)

    dma("y", [], ["cpF"], (T.CPI[:, 256:384], T.suf[:, :]))
    dma("s", [], ["cpT"], (T.CPI[:, 0:128], T.tab[0:128:16, :]))
    dma("y", [], ["cpL"], (T.CPI[:, 128:256], T.lnk[:, :]))
    for k in range(4):
        dma("s" if k % 2 == 0 else "y", [], ["tab%d" % k], (T.tabI[:, 512 * k:512 * k + 512], T.tab[:, 512 * k:512 * k + 512]))
    dma("y", [], ["CXI"], (z("CXI"), T.cx[:, :]))

    def iota(tile, key, pattern, base, cm, **kw):
        op("q", [], [key], lambda e: e.iota(tile, pattern, base, cm, **kw))
    fl = {"allow_small_or_imprecise_dtypes": True}
    iota(z("i_rm"), "i_rm", [[-1, 16]], 0, 1)
    iota(z("i_g8"), "i_g8", [[-16, 8]], 0, 1)
    iota(z("i_bm"), "i_bm", [[-16, 8], [0, 16]], 0, 1)
    iota(z("i_dp"), "i_dp", [[1, 128]], 0, -1)
    iota(z("i_sf"), "i_sf", [[1, 128]], -15, -16)
    iota(T.CPI[:, 384:512], "cpj", [[1, 128]], 0, 128)
    iota(T.CPI[:, 512:544], "cpk", [[1, 32]], 0, 32)
    iota(z("i_pc"), "i_pc", [[0, 16]], 0, 1)
    iota(z("JI"), "JI", [[16, 96]], 0, 0, **fl)
    iota(z("i_wr"), "i_wr", [[1, 128]], 0, 0)
    for i in range(10):
        iota(T.BIT[:, 1024 * i:1024 * i + 1024], "bit%d" % i, [[0, 1024 >> (i + 1)], [1, 2], [0, 1 << i]], 0, 0, **fl)

    SR, BA = OP.logical_shift_right, OP.bitwise_and
    V([], ["AUX"], ms(T.AUX[:, :], 0.0))
    V([], ["COMB"], ms(T.COMB[:, :], 0.0))
    V([], ["COMBX"], ms(T.COMBX[:, :], 0.0))
    tz("i_rm", "i_rm", 15, BA)
    tz("i_g8", "i_g8", 4, OP.arith_shift_right)
    tz("i_bm", "i_bm", 4, OP.arith_shift_right)
    tz("RM", "i_rm", 0.0, OP.is_equal)
    tz("G8", "i_g8", 0.0, OP.is_equal)
    tz("BM", "i_bm", 0.0, OP.is_equal)
    tz("U1", "i_dp", -1.0, OP.is_equal)
    tz("IDN", "i_dp", 0.0, OP.is_equal)
    tz("LTu", "i_dp", 0.0, OP.is_ge)
    t2("U1", "U1", "BM", OP.mult)
    V(["G8", "COMBX"], ["COMBX"], cp(T.COMBX[:, 15:143:16], z("G8")))
    tz("SELF", "i_sf", 0.0, OP.is_equal, 32.0, OP.mult)
    tz("SF2", "i_sf", -128.0, OP.is_equal)
    t2("SH32", "U1", "IDN", OP.subtract)
    t2("SELF", "SELF", "SF2", OP.add)
    t2("LTB", "LTu", "BM", OP.mult)
    V([], ["ONES"], ms(z("ONES"), 1.0))
    V([], ["WTz"], ms(T.WT[:, 2048:NW], 0.0))
    V([], ["DTz"], ms(T.DT[:, 2048:2304], 0.0))
    V([], ["DL"], ms(z("DL"), 0.0))
    ncol = [0]

    def column(terms):
        prev, key = None, None
        for r, wt in terms:
            c = ncol[0]
            ncol[0] += 1
            out = z("COLS", c, c + 1)
            kw = {"bias": prev} if key else {}
            S(["RM"] + ([key] if key else []), ["col%d" % c], ac(out, RMc(r), AF.Identity, scale=float(wt), **kw))
            prev, key = out, "col%d" % c
        return prev, key

    def make_comb(v, col, key):
        S([key, "G8", "COMB"], ["cb%d" % v], ac(T.COMB[:, v * 144 + 15:v * 144 + 143:16], z("G8"), AF.Copy, scale=col))

    def scaled(out, a, col, key):
        S([a, key], [out], ac(z(out), z(a), AF.Copy, scale=col))

    colB, kB = column([(4, 1), (9, 1)])
    S(["AUX", kB], ["AUX"], ac(T.AUX[:, 0:2304], T.AUX[:, 0:2304], AF.Identity, bias=colB))
    colR, kR = column([(15, 4096)])
    S(["AUX", "RM"], ["AUX"], ac(T.AUX[:, 2304:NW], T.AUX[:, 2304:NW], AF.Identity, bias=RMc(4)))
    S(["AUX", kR], ["AUX"], ac(T.AUX[:, 0:1], T.AUX[:, 0:1], AF.Identity, bias=colR))
    colF, kF = column([(15, -1152 - 4128)])
    make_comb(CF, *column([(4, -1152 - 4128), (5, 32), (6, 1)]))
    make_comb(CA, *column([(0, 32), (1, 1), (4, -4128)]))
    make_comb(CE, RMc(15), "RM")
    scaled("NI", "IDN", -1.0, "IDN")
    scaled("LT", "LTB", 256.0, "LTB")
    scaled("R15", "IDN", RMc(15), "RM")
    scaled("ESC", "BM", *column([(15, -32)]))

    b32 = 129.0 - 31.0 / 64
    V(["cpj"], ["cpj"], ts(T.CPI[:, 384:512], T.CPI[:, 384:512], 2047, BA))
    V(["cpk"], ["cpk"], ts(T.CPI[:, 512:544], T.CPI[:, 512:544], 511, BA))
    V(["cpF", "cpL"], ["HBa"], ts(z("HB", 128, 384), T.CPI[:, 128:384], 1.0 / 32, OP.mult, b32, OP.add))
    V(["cpT"], ["cpl0"], ts(T.CPL[:, 0:128], T.CPI[:, 0:128], 4, SR, 31, BA))
    V(["cpF", "cpL", "cpj", "cpk"], ["cpl1"], ts(T.CPL[:, 128:544], T.CPI[:, 128:544], 31, BA))
    V(["cpT"], ["HBb"], ts(z("HB", 0, 128), T.CPI[:, 0:128], 1.0 / 512, OP.mult, 129.0 - 511.0 / 1024, OP.add))
    V(["cpl0", "cpl1"], ["LB"], cp(z("LB"), T.CPL[:, :]))
    dma("y", ["HBa"], ["fb0"], (T.FB[0:8, :], z("HB", 256, 384)))
    dma("y", ["LB"], ["fb1"], (T.FB[8:16, :], z("LB", 256, 384)))
    V(["cpj"], ["HBc"], ts(z("HB", 384, 512), T.CPI[:, 384:512], 1.0 / 32, OP.mult, b32, OP.add))
    V(["cpk"], ["HBd"], ts(z("HB", 512, 544), T.CPI[:, 512:544], 1.0 / 32, OP.mult, b32 + 64.0, OP.add))
    for j, (r, key, t, a) in enumerate(((5, "HBa", "HB", 256), (6, "LB", "LB", 256), (0, "HBb", "HB", 0), (1, "LB", "LB", 0),
                                        (2, "HBa", "HB", 128), (3, "LB", "LB", 128), (7, "HBc", "HB", 384), (8, "LB", "LB", 384))):
        dma("y", [key, "AUX"], ["ar%d" % j], (T.AUX[r:128:16, 0:2048], z(t, a, a + 128)))
    dma("y", ["HBd", "AUX"], ["ar8"], (T.AUX[7:128:16, 2048:NW], z("HB", 512, 544)))
    dma("y", ["LB", "AUX"], ["ar9"], (T.AUX[8:128:16, 2048:NW], z("LB", 512, 544)))
    for key, a, b in (("vv0", 0, 1536), ("vv1", 1536, 6144), ("vv2", 6144, 12288)):
        dma("y", [], [key], *[(T.VV[i:128:16, a:b], T.vv[:, a:b]) for i in range(16)])

    for k in range(4):
        a, b = 512 * k, 512 * k + 512
        V(["tab%d" % k], ["yb%d" % k], ts(T.YB[:, a:b], T.tabI[:, a:b], -7.5, OP.add, 201326592.0, OP.add))
        V(["tab%d" % k], ["ci%d" % k], ts(T.CI[:, a:b], T.tabI[:, a:b], 15, BA))
        S(["yb%d" % k], ["st%d" % k], ac(T.ST[:, a:b], T.YB[:, a:b], AF.Identity, bias=-12584064.0, scale=0.0625))
    pieces = [(k, 512 * k, PX[k // 2][:, 1024 * (k % 2):1024 * (k % 2) + 512], (PK0 if k % 2 == 0 else PK2)[k // 2]) for k in range(4)]
    o = WHERE["SELF"][1]
    for k, a, P, pk in pieces:
        PE(["st%d" % k, "SH32", "SELF", "fb0", "fb1"], [pk], mm(P, z("SH32"), T.ST[:, a:a + 512], True, False),
           mm(P, T.zb[0:16, o:o + 128], T.FB[0:16, a:a + 512], False, True))
        V(["ci%d" % k], ["w1%d" % k], ts(T.W1[:, a:a + 512], T.CI[:, a:a + 512], 1.03, OP.mult, 128.48, OP.add))
        V(["w1%d" % k], ["wt%d" % k], ts(T.WT[:, a:a + 512], T.W1[:, a:a + 512], -128.0, OP.add))
    for k, a, P, pk in pieces:
        S([pk, kF], ["dt%d" % k], ac(T.DT[:, a:a + 512], P, AF.Identity, bias=colF))
    V(["CXI"], ["c0_0", "c0_1"], cp(T.CL[:, 0:96], z("CXI")))
    WTK = ["WT", "WTz"] + ["wt%d" % k for k in range(4)]
    DTK = ["DT", "DTz"] + ["dt%d" % k for k in range(4)]
    STK = ["STz"] + ["st%d" % k for k in range(4)]
    cR, nkR = column([(15, -1)])
    S([nkR], ["d0c"], ac(z("d0c"), cR, AF.Identity, bias=1.0))
    S(["d0c", "dt0"], ["dt0"], ac(T.DT[:, 0:1], T.DT[:, 0:1], AF.Copy, scale=z("d0c")))

    def zeros():
        dma("y", ["ZB", "VW"], ["VW"], (T.VW[:, 0:384], T.ZB[:, 0:384]))
        dma("y", ["ZF", "SW"], ["SW"], (T.SW[:, 0:384], z("ZF", 0, 384)))
        dma("y", ["ZB", "LW"], ["LW"], (T.LW[:, 0:1536], T.ZB[:, :]))

    def late_a():
        V([], ["HT"], ms(z("HT"), 0.0))
        V([], ["ZB"], ms(T.ZB[:, :], 0.0))
        V([], ["ZF"], ms(z("ZF"), 0.0))
        dma("y", ["ZB"], ["LBA"], (T.LBA[:, :], T.ZB[:, 0:H]))
        dma("y", ["ZF"], ["STz"], (T.ST[:, 2048:NW], z("ZF")))
        zeros()
        V([], ["OB"], ms(z("OB"), 0.0))
        V([], ["CS"], ms(z("CS", 0, 8), 0.0))
        V([], ["Z96"], ms(z("Z96"), 0.0))
        tz("i_pc", "i_pc", 15, BA)
        tz("TRI", "i_dp", 0.0, OP.is_le, 8192.0, OP.mult)
        tz("U2", "i_dp", 1.0, OP.is_equal)
        V(["OB"], ["OB"], ms(z("OB", 112, 128), 1.0))
        V(["i_pc"], ["PC"], cp(z("PC"), z("i_pc", 0, 1)))
        tz("WR", "i_wr", 896.0, OP.add)
        V(["SH32"], ["SH16"], cp(z("SH16"), z("SH32")))
        t2("U2", "U2", "BM", OP.mult)
        t2("BID", "U2", "IDN", OP.subtract)

    late, todo = {}, []

    def drain(m):
        for _ in range(min(m, len(todo))):
            todo.pop(0)()

    def later(f, *a):
        todo.append(lambda: f(*a))

    def shifted(out, a, na, c, o=0):
        S([a, "PC"], [out], ac(z(out, o, o + na), z(a, 0, na), AF.Identity, bias=c))

    def later_comb(v, terms):
        later(lambda: make_comb(v, *column(terms)))

    def key_tiles(gg):
        for tile, kt in (("SELK", "K8"), ("NSELK", "NK8")):
            S(["ONES", kt], [tile + str(gg)], ac(T[tile][:, 128 * gg:128 * gg + 128], z("ONES"), AF.Copy, scale=z(kt, gg, gg + 1)))

    def lane_bits():
        S(["LBA", "RM"], ["LBA"], ac(T.LBA[:, :], T.LBA[:, :], AF.Identity, bias=RMc(15)))
        for i in range(10):
            dma("y", ["bit%d" % i, "LBA"], ["lb%d" % i], (T.LBA[i:128:16, :], T.BIT[0:8, 1024 * i:1024 * i + H]))

    def slot_combs():
        sa = column([(i, 1 << i) for i in range(10)] + [(15, 2048)])
        make_comb(CSA, *sa)
        c = ncol[0]
        ncol[0] += 1
        S(["RM", sa[1]], ["colx"], ac(z("COLS", c, c + 1), RMc(15), AF.Identity, bias=sa[0], scale=768.0))
        make_comb(CSB, z("COLS", c, c + 1), "colx")

    LBK = ["LBA"] + ["lb%d" % i for i in range(10)]

    def keep():
        late["keep"] = column([(0, 1), (1, 1), (2, 1), (3, 1)])
    later(shifted, "JL", "JI", 96, z("PC"))
    later(shifted, "J2", "JL", 96, -1663.0)
    later(shifted, "J3", "JL", 96, 384.0)
    later(shifted, "JD", "JL", 24, 1536.0)
    later(shifted, "JD2", "JL", 24, 3584.0)
    for t in range(2):
        later(shifted, "DUM%d" % t, "JL", 8, 2304.0 + 128 * t)
        later(shifted, "DUM%d" % t, "JL", 8, 2304.0 + 128 * t, 8)
    later(scaled, "E0", "IDN", RMc(0), "RM")
    later(scaled, "ID2", "IDN", 2.0, "IDN")
    later(scaled, "NI2K", "IDN", -2048.0, "IDN")
    later(lambda: scaled("CANDM", "BM", *column([(9, -1)])))
    later_comb(CLK, [(2, 32), (3, 1), (4, -32)])
    later_comb(CID, [(4, -1152 - 4128), (7, 32), (8, 1)])
    for v, r in ((C0, 0), (C7, 7), (C8, 8)):
        later(make_comb, v, RMc(r), "RM")
    later(lambda: scaled("K8", "G8", *column([(7, 32), (8, 1)])))
    later(scaled, "NK8", "K8", -1.0, "K8")
    later(lane_bits)
    later(lambda: scaled("N01", "NI", *column([(0, 1), (1, 1)])))
    later(keep)
    for gg in range(8):
        later(key_tiles, gg)
    later(slot_combs)
    later(lambda: S(LBK, ["LBB"], ac(T.LBB[:, :], T.LBA[:, :], AF.Identity, bias=-200.0, scale=400.0)))

    def lists(p, idx):
        return T.CL[:, idx * 96 + 48 * p:idx * 96 + 48 * p + 48], "c%d_%d" % (idx, p)

    def p1(p, idx, k):
        off, ck = lists(p, idx)
        P = PX[p]
        S(AUXK + [ck], ["x%d" % p], ac(x[p][:, :], T.AUX[:, 0:2304].indirect(off), AF.Copy))
        wi = T.WT[:, 0:2304].indirect(off)
        V(WTK + [ck] + (["m%d" % p] if k else []), ["w%d" % p],
          tt(w[p][:, :], wi, T.MM[:, H * p:H * p + H], OP.mult) if k else cp(w[p][:, :], wi))
        PE(["w%d" % p, "BM"], [PK0[p]], mm(P[:, 0:512], z("BM"), w[p][:, 0:512], True, True),
           mm(P[:, 512:768], z("BM"), w[p][:, 512:768], True, True))
        PE(["x%d" % p, "cb%d" % CA], [LK[p]],
           *[mm(LP[p][:, 0:48], comb(CA, i), x[p][:, i:H:16], i == 0, False) for i in range(16)])
        S(["w%d" % p], ["n%d" % p], ac(n[p][:, :], w[p][:, :], AF.Relu, bias=-1.0))
        PE(["x%d" % p, "n%d" % p, "R15", "LT"], [PK0[p], PK2[p]],
           mm(P[:, 768:1024], z("R15"), x[p][:, 0:256], True, False), mm(P[:, 768:1024], z("LT"), n[p][:, 0:256], False, True),
           mm(P[:, 1024:1536], z("R15"), x[p][:, 256:768], True, False), mm(P[:, 1024:1536], z("LT"), n[p][:, 256:768], False, True))

    def p2(p, idx, k):
        off, ck = lists(p, idx)
        P, s = PX[p], k % SP
        vk = "vv%d" % (0 if k == 0 else 1 if k < 4 else 2)
        V([vk, PK0[p]], ["Y%d" % p], tt(Y[p][:, :], T.VV[:, k * 1536 + H * p:k * 1536 + H * p + H], P[:, 0:768], OP.mult))
        V(["Y%d" % p, PK0[p], PK2[p]], ["k%d" % p], tt(cond[p][:, :], P[:, 768:1536], Y[p][:, :], OP.is_le))
        V(DTK + [ck, "k%d" % p], ["X%d" % p], tt(X[p][:, :], T.DT[:, 0:2304].indirect(off), cond[p][:, :], OP.mult))

        def esc_list():
            if s == SP - 1:
                PE(["k%d" % p, "cb%d" % CE], [PK2[p]],
                   *[mm(P[:, 1024:1072], comb(CE, i), cond[p][:, i:H:16], i == 0, i == 15) for i in range(16)])
            elif p == 0:
                PE(["k0", "cb%d" % CE], [PK2[0]],
                   *[mm(P[:, 1024:1032], comb(CE, i), cond[0][:, i:128:16], i == 0, i == 15) for i in range(16)])
                S([PK2[0]], ["HT"], ac(z("HT", s + 2, 40, 5), P[:, 1024:1032], AF.Copy))

        def marks():
            if k == RO * SP - 1:
                return
            f = []
            for a, b in ((0, 512), (512, 768)):
                if k:
                    f.append(mm(P[:, a:b], z("IDN"), T.MM[:, H * p + a:H * p + b], True, False))
                f += [mm(P[:, a:b], z("NI"), w[p][:, a:b], k == 0, False), mm(P[:, a:b], z("ESC"), cond[p][:, a:b], False, True)]
            PE(["w%d" % p, "k%d" % p, "IDN", "NI", "ESC"] + (["m%d" % p] if k else []), [PK0[p]], *f)
            S([PK0[p]], ["m%d" % p],
              ac(T.MM[:, H * p:H * p + H], P[:, 0:768], AF.Sigmoid, bias=8064.0 if k else 8320.0, scale=256.0))

        def xlist():
            PE(["X%d" % p, "COMBX"], [LK[p]],
               *[mm(LP[p][:, 0:48], combx(i), X[p][:, i:H:16], False, i == 15) for i in range(16)])
        if s < SP - 1:
            marks()
            xlist()
            esc_list()
            return None
        esc_list()
        xlist()
        return marks

    def v5(p, idx, rnd):
        off, ck = lists(p, idx)
        if rnd == 0:
            V([LK[p]], [ck], cp(off, LP[p][:, 0:48]))
        else:
            t = z("CIT", 48 * p, 48 * p + 48)
            V([LK[p]], ["cit%d" % p], cp(t, LP[p][:, 0:48]))
            V(["cit%d" % p], ["cit%d" % p], ts(t, t, 4095, BA))
            V(["cit%d" % p], [ck], cp(off, t))

    nxt = T.cores[(rank + 1) % len(T.cores)]
    rid, pid = topo.addr(nxt, core)
    rmask, ne = topo.mask(core, nxt), len(topo.engines(core, nxt))

    for rnd in range(RO):
        base = 5 * rnd
        for s in range(SP):
            k, idx = rnd * SP + s, base + s
            for p in (0, 1):
                if s:
                    v5(p, idx, rnd)
                p1(p, idx, k)
                drain(7 if k and p else 0)
            if k == 0:
                late_a()
            V(["c%d_0" % idx], ["DL"], cp(z("DL", s + 1, 40, 5), T.CL[:, idx * 96:idx * 96 + 8]))
            for p in (0, 1):
                mk = p2(p, idx, k)
                if mk and p == 0:
                    mk()
                drain(4 if p == 0 else 0)
            if k == SP:
                zeros()
        drain(len(todo))
        i4 = base + SP
        LA, LB = T.LAp, T.LBp
        nl = T.CL[:, i4 * 96:i4 * 96 + 8]
        nk = "c%d_0" % i4
        V([PK2[0]], ["E16a"], cp(z("E16", 0, 48), T.PA[:, 1024:1072]))
        v5(0, i4, rnd)
        V([PK2[1]], ["E16b"], cp(z("E16", 48, 96), T.PB[:, 1024:1072]))
        v5(1, i4, rnd)
        PE(["E16a", "E16b", "LTB", "NI2K", "BM"], ["#LA"], mm(LA[:, 128:224], z("LTB"), z("E16"), True, False),
           mm(LA[:, 128:224], z("NI2K"), z("E16"), False, True), mm(LA[:, 256:352], z("BM"), z("E16"), True, True))
        off, ck = lists(0, i4)
        S(AUXK + [ck], ["A20"], ac(T.A2[:, 0:H], T.AUX[:, 0:2304].indirect(off), AF.Copy))
        mk()
        off, ck = lists(1, i4)
        S(AUXK + [ck], ["A21"], ac(T.A2[:, H:1536], T.AUX[:, 0:2304].indirect(off), AF.Copy))
        DUM = "DUM%d" % rnd
        t2("hd", "HT", "DL", OP.mult)
        V(["HT", "E16a"], ["CAND"], tt(z("CAND", 0, 8), z("HT", 4, 40, 5), z("E16", 0, 8), OP.is_gt),
          tt(z("CAND", 8, 16), z("HT", 4, 40, 5), z("E16", 0, 8), OP.is_gt))
        t2("d1", "DL", "hd", OP.subtract)
        V(["#LA", "Z96", "CS"], ["CS1"],
          lambda e: e.tensor_tensor_scan(z("CS", 1, 97), LA[:, 256:352], z("Z96"), 0.0, OP.add, OP.add))
        V(["#LA", "CS", "CS1"], ["CNT"], tt(z("CNT"), LA[:, 128:224], z("CS", 0, 96), OP.add))
        tz("OKT", "CNT", -1663.5, OP.is_le)
        t2("TT", "CNT", "J2", OP.subtract)
        t2("TT2", "TT", "OKT", OP.mult)
        t2("POSF", "TT2", "J3", OP.add)
        V(["POSF"], ["POS"], cp(z("POS"), z("POSF")))
        S(["LBB", "POS", "SW"], ["SW"], ac(T.SW[:, :].indirect(z("POS", 48, 96)), T.LBB[:, :], AF.Sigmoid))
        V(LBK + ["POS", "VW"], ["VW"], cp(T.VW[:, :].indirect(z("POS", 0, 48)), T.LBA[:, :]))
        PE(["VW", "cb%d" % CSA], ["#LA"],
           *[mm(LA[:, 384:408], comb(CSA, i), T.VW[:, i:384:16], i == 0, False) for i in range(16)])
        S(["SW"], ["SWb"], ac(z("SWb"), T.SW[:, 0:384], AF.Copy))
        PE(["SWb", "cb%d" % CSB], ["#LA"],
           *[mm(LA[:, 384:408], comb(CSB, i), z("SWb", i, 384, 16), False, i == 15) for i in range(16)])
        V(["HT", "d1"], ["FS"], lambda e: e.tensor_tensor_scan(z("FS"), z("HT"), z("d1"), 0.0, OP.mult, OP.add))
        V(["FS", "DL", DUM], ["KT"], tt(z("KT", 0, 8), z("FS", 3, 40, 5), z(DUM, 0, 8), OP.subtract),
          tt(z("KT", 8, 16), z("DL", 4, 40, 5), z(DUM, 0, 8), OP.subtract))
        t2("KT2", "KT", "CAND", OP.mult)
        t2("KK", "KT2", DUM, OP.add)
        V(["KK"], ["FK"], cp(z("FK"), z("KK")))
        S(AUXK + ["FK"], ["XF"], ac(z("XF"), T.AUX[:, :].indirect(z("FK")), AF.Copy))
        SND, RCV = T["SND%d" % rnd], T["RCV%d" % rnd]
        sk, rk = "SND%d" % rnd, "RCV%d" % rnd
        V(["#LA"], ["LNE"], ts(z("LNE"), LA[:, 384:408], -2048.0, OP.add, 0.0, OP.max))
        V(["#LA"], ["T1"], ts(z("T1"), LA[:, 384:408], 2047.5, OP.is_ge))
        V(["#LA"], [sk + "b"], ts(SND[:, 384:408], LA[:, 384:408], 2047.5, OP.is_ge))
        S(["A20", "A21", "LNE"], [sk + "a"], ac(SND[:, 0:384], T.A2[:, :].indirect(z("LNE")), AF.Copy))
        width = 408
        if rnd == 0:
            V(["m0", "m1", "LNE"], [sk + "c"], cp(SND[:, 408:792], T.MM[:, 0:1536].indirect(z("LNE"))))
            width = 792
        do_waits("q", [sk + c for c in "abc"[:2 if rnd else 3]], [])
        g.remote_dma(RCV[:, 0:width], SND[:, 0:width], T.sem["arr%d" % rnd], T.sem["snt%d" % rnd], pid, rid, rmask)
        used["snt%d" % rnd] = ne
        used["arr%d" % rnd] = ne
        record(("rem%d" % rnd, "arr%d" % rnd, ne, {}), [], [rk])
        V(["#LA", "JD2"], ["LNF"], tt(z("LNF"), LA[:, 384:408], z("JD2"), OP.subtract))
        S(WTK + [nk], ["ug"], ac(z("ug"), T.WT[:, 0:2304].indirect(nl), AF.Copy))
        t2("PRE", "LNF", "T1", OP.mult)

        for h in (0, 1):
            f = []
            xf = z("XF", 128 * h, 128 * h + 128)
            for gg in range(8):
                o = PX[h][:, 128 * gg:128 * gg + 128]
                f += [mm(o, T.SELK[:, 128 * gg:128 * gg + 128], xf, True, False),
                      mm(o, xf, T.NSELK[:, 128 * gg:128 * gg + 128], False, False), mm(o, z("IDN"), z("TRI"), False, True)]
            PE(["XF", "IDN", "TRI"] + [c + "SELK%d" % i for i in range(8) for c in ("", "N")], [PK0[h]], *f)
        V(["#A0"], ["EQF"], ts(T.EQF[:, :], T.PA[:, 0:1024], 0.0, OP.is_equal))
        S(["#B0"], ["ABD"], ac(T.ABD[:, :], T.PB[:, 0:1024], AF.Abs))
        S(["ABD"], ["EQD"], ac(T.EQD[:, :], T.ABD[:, :], AF.Relu, bias=1.0, scale=-1.0))
        oh = LB[:, 256:384]
        PE(["k0", "BID", "E0", "ONES"], ["#LB"], mm(oh, z("BID"), cond[0][:, 0:128], True, False), mm(oh, z("E0"), z("ONES"), False, True))

        def dup(h, EQ, ek):
            o = PX[h][:, 1024:1152]
            PE([ek, "OB", "XF", "CANDM"], [PK2[h]],
               *([mm(o, z("OB", 112 - 16 * gg, 240 - 16 * gg), EQ[:, 128 * gg:128 * gg + 128], gg == 0, False) for gg in range(8)]
                 + [mm(o, z("CANDM"), z("XF", 128 * h, 128 * h + 128), False, True)]))

        def winners(h):
            P = PX[h]
            V([PK2[h]], ["AR%d" % h], ts(z("AR", 128 * h, 128 * h + 128), P[:, 1024:1152], -0.5, OP.is_lt))
            PE(["AR%d" % h, "cb%d" % C0], [PK2[h]],
               *[mm(P[:, 1280:1288], comb(C0, i), z("AR", 128 * h + i, 128 * h + 128, 16), i == 0, i == 15) for i in range(16)])

        def offsets(h, o1, o2, off):
            V([PK2[h], "KT2"], [o1], tt(z(o1), PX[h][:, 1280:1288], z("KT2", 8 * h, 8 * h + 8), OP.mult))
            V([o1, DUM], [o2], tt(z(o2), z(o1), z(DUM, 0, 8), OP.add))
            V([o2], [off], cp(z(off), z(o2)))
        dup(0, T.EQF, "EQF")
        winners(0)
        V(["#LB", "AR0"], ["OA"], tt(z("OA"), oh, z("AR", 0, 128), OP.mult))
        S(["OA"], ["nOA"], ac(z("nOA"), z("OA"), AF.Identity, bias=1.0, scale=-1.0))
        scaled("OA2", "OA", 2.0, "OA")
        offsets(0, "AO", "AO2", "OFF")
        dup(1, T.EQD, "EQD")
        wc = 2048 + 128 * rnd
        tz("i_u", "ug", 0.53, OP.mult, 0.45, OP.add)
        V(WTK + ["OFF", "nOA"], ["tg"], tt(z("tg"), T.WT[:, :].indirect(z("OFF")), z("nOA"), OP.mult))
        winners(1)
        if rnd == 0:
            V(STK + ["OFF", "nOA"], ["tS"], tt(z("tS"), T.ST[:, :].indirect(z("OFF")), z("nOA"), OP.mult))
            t2("qS", "OA", "WR", OP.mult)
            V(STK + [nk], ["Sc"], cp(z("Sc"), T.ST[:, 0:2304].indirect(nl)))
            S(AUXK + [nk], ["XC"], ac(z("XC"), T.AUX[:, 0:2304].indirect(nl), AF.Copy))
            o = T.PA[:, 1408:1536]
            PE(["SH16", "tS", "qS", "XF", "cb%d" % CF], ["#A2"], mm(o, z("SH16"), z("tS"), True, False),
               mm(o, z("SH16"), z("qS"), False, False), mm(o, comb(CF, 15), z("XF", 0, 128), False, True))
            PE(["OA", "cb%d" % C0], ["#A0"], mm(T.PA[:, 0:128], comb(C0, 0), z("OA"), True, False),
               mm(T.PA[:, 0:128], comb(C0, 1), z("OA"), False, True))
            o = T.PB[:, 0:128]
            PE(AUXK + ["XF", "N01", "cb%d" % C7, "cb%d" % C8], ["#B0"], mm(o, comb(C7, 0), T.AUX[:, 2048:2176], True, False),
               mm(o, comb(C8, 1), T.AUX[:, 2048:2176], False, False), mm(o, z("N01"), z("XF", 0, 128), False, True))
            o = T.PB[:, 1408:1536]
            PE(["SH16", "Sc", "XC", "cb%d" % CID], ["#B2"], mm(o, z("SH16"), z("Sc"), True, False),
               mm(o, comb(CID, 15), z("XC"), False, True))
            S(["#A2"], ["xs"], ac(z("xs"), T.PA[:, 1408:1536], AF.Copy))
            S(["#A0"], ["FLs"], ac(z("FLs"), T.PA[:, 0:128], AF.Copy))
            S(["#B2"], DTK, ac(T.DT[:, 2048:2176], o, AF.Copy))
            scaled("xt", "XC", *late["keep"])
        V(["tg", "OA2", "OFF"], WTK, tt(T.WT[:, :].indirect(z("OFF")), z("tg"), z("OA2"), OP.add))
        V(["#LB", "AR1"], ["OBm"], tt(z("OBm"), oh, z("AR", 128, 256), OP.mult))
        PE(["OBm", "ID2"], ["#LA"], mm(LA[:, 256:384], z("ID2"), z("OBm"), True, True))
        offsets(1, "BO", "BO2", "OFD")
        if rnd == 0:
            tz("i_k", "xs", 1.0 / 4096, OP.mult)
            V(["FLs", "#B0"], ["fd"], tt(z("fd"), z("FLs"), T.PB[:, 0:128], OP.mult))
            tz("kk", "i_k", -4096.0, OP.mult)
        V(WTK + ["OFD", "OBm"], ["s1"], tt(z("s1"), T.WT[:, :].indirect(z("OFD")), z("OBm"), OP.add))
        if rnd == 0:
            V(["XF", "fd", "OFF"], AUXK, tt(T.AUX[:, :].indirect(z("OFF")), z("XF", 0, 128), z("fd"), OP.add))
        V(["s1", "#LA"], ["s2"], tt(z("s2"), z("s1"), LA[:, 256:384], OP.max))
        if rnd == 0:
            V(["kk", "xs", "OFF"], DTK, tt(T.DT[:, :].indirect(z("OFF")), z("kk"), z("xs"), OP.add))
        tz("s3", "s2", 16.0, OP.min)
        if rnd == 0:
            V(["xt"] + AUXK, AUXK, tt(T.AUX[:, 2048:2176], z("xt"), T.AUX[:, 2048:2176], OP.add))
        V(["s3", "OFD"], WTK, cp(T.WT[:, :].indirect(z("OFD")), z("s3")))
        V(["i_u", "AR0"], WTK, tt(T.WT[:, wc:wc + 128], z("i_u"), z("AR", 0, 128), OP.mult))
        V([nk, "c%d_1" % i4], ["CLF"], cp(z("CLF"), T.CL[:, i4 * 96:i4 * 96 + 96]))

        def counts_out(a, b, q):
            V(WTK, ["yn%d" % a], ts(T.YN[:, a:b], T.WT[:, a:b], -1.0, OP.add, 0.0, OP.max))
            dma(q, ["yn%d" % a], [], (T.yn[:, a:b], T.YN[:, a:b]))
        if rnd == RO - 1:
            counts_out(0, 1152, "s")
        V([rk, "PRE"], ["RX1"], tt(z("RX1"), RCV[:, 384:408], z("PRE"), OP.mult))
        t2("RX2", "RX1", "JD", OP.add)
        V(["RX2"], ["TO"], cp(z("TO"), z("RX2")))
        V([rk, "TO", "LW"], ["LW"], cp(T.LW[:, :].indirect(z("TO")), RCV[:, 0:384]))
        PE(["LW", "cb%d" % CLK], ["#LB"], *[mm(LB[:, 128:224], comb(CLK, i), T.LW[:, i:1536:16], i == 0, i == 15) for i in range(16)])
        if rnd == 0:
            V([rk, "TO", "m0", "m1"], ["m0", "m1"], cp(T.MM[:, :].indirect(z("TO")), RCV[:, 408:792]))
        else:
            counts_out(1152, 2304, "s")
        V(["#LB", "CLF"], ["cit0", "cit1"], tt(z("CIT"), LB[:, 128:224], z("CLF"), OP.max))
        V(["cit0", "cit1"], ["cit0", "cit1"], ts(z("CIT"), z("CIT"), 4095, BA))
        if rnd < RO - 1:
            V(["cit0", "cit1"], ["c%d_0" % (i4 + 1), "c%d_1" % (i4 + 1)], cp(T.CL[:, (i4 + 1) * 96:(i4 + 2) * 96], z("CIT")))
            V(["#LB"], ["HF"], ts(z("HF"), LB[:, 128:136], 4095.5, OP.is_ge))
            V(["FS"], ["DL"], cp(z("DL", 0, 40, 5), z("FS", 4, 40, 5)))
            V(["HF", "E16a"], ["HT"], tt(z("HT", 1, 40, 5), z("E16", 0, 8), z("HF"), OP.subtract))
        else:
            V(["cit0", "cit1"], ["YC"], cp(z("YC"), z("CIT")))
            dma("y", ["YC"], [], (T.yc[:, :], z("YC")))

    for q in ("v", "s", "t", "q"):
        g.wait_ge(T.sem[q], cnt[q])
    for name, val in used.items():
        g.wait_ge(T.sem[name], val)
